import numpy as np
import ml_dtypes


def mxq(x, axis, fmt="e4m3"):
    dtype, down = {"e4m3": (ml_dtypes.float8_e4m3fn, 7), "e5m2": (ml_dtypes.float8_e5m2, 14)}[fmt]
    v = np.moveaxis(np.asarray(x, np.float32).astype(ml_dtypes.bfloat16).astype(np.float64), axis, -1)
    blocks = v.reshape(v.shape[:-1] + (-1, 32))
    amax = np.abs(blocks).max(-1, keepdims=True)
    byte = np.maximum(np.where(amax > 0, np.frexp(amax)[1] - 1 + 127, 0) - down, 1)
    scale = np.exp2(byte - 127.0)
    codes = (blocks / scale).astype(np.float32).astype(dtype).astype(np.float64)
    return np.moveaxis((codes * scale).reshape(v.shape), -1, axis)


WIDE = False


def mx_kscale(k):
    if not WIDE:
        return np.ones(k)
    levels = np.array([10, -10, 5, -5, 0])
    if k % 512:
        return np.exp2(np.random.permutation(np.resize(levels, k // 32))).repeat(32)
    a = np.empty((k // 512, 16))
    for p in range(k // 512):
        a[p, :8] = np.random.permutation(np.resize(levels, 8))
        for g in range(8):
            far = levels[np.abs(levels - a[p, g]) >= 10]
            a[p, g + 8] = far[np.random.randint(len(far))]
    return np.exp2(a.ravel()).repeat(32)


BF16 = ml_dtypes.bfloat16


def bf(x):
    return np.asarray(x, np.float32).astype(BF16)


def f64(x):
    return np.asarray(x).astype(np.float64)


E2M1 = np.array([0.0, 0.5, 1.0, 1.5, 2.0, 3.0, 4.0, 6.0, -0.0, -0.5, -1.0, -1.5, -2.0, -3.0, -4.0, -6.0])


def pack_weight(w, fmt):
    k, n = w.shape
    w = f64(bf(w)).reshape(k // 32, 32, n)
    amax = np.abs(w).max(1)
    if fmt == "e4m3":
        byte = np.frexp(amax)[1] - 1 + 127 - 7
    else:
        mant, ex = np.frexp(amax / 6.0)
        byte = np.where(mant > 0.5, ex, ex - 1) + 127
    byte = np.clip(np.where(amax > 0, byte, 1), 1, 254)
    scaled = (w * np.exp2(127.0 - byte)[:, None, :]).reshape(k, n).astype(np.float32)
    by_word = np.ascontiguousarray(scaled.reshape(k // 512, 128, 4, n).transpose(0, 1, 3, 2))
    if fmt == "e4m3":
        words = by_word.astype(ml_dtypes.float8_e4m3fn).view(np.uint8)
    else:
        c = by_word.astype(ml_dtypes.float4_e2m1fn).view(np.uint8) & 0xF
        words = c[..., 0::2] | (c[..., 1::2] << 4)
    return np.ascontiguousarray(words), np.ascontiguousarray(byte.astype(np.uint8).reshape(k // 512, 16, n))


def unpack_weight(words, scales, fmt):
    g, p, n, _ = words.shape
    if fmt == "e4m3":
        vals = np.ascontiguousarray(words).view(ml_dtypes.float8_e4m3fn).astype(np.float64)
    else:
        nib = np.empty((g, p, n, 4), np.uint8)
        nib[..., 0::2] = words & 0xF
        nib[..., 1::2] = words >> 4
        vals = E2M1[nib]
    vals = vals * np.repeat(np.exp2(scales.astype(np.float64) - 127.0), 8, axis=1)[..., None]
    return vals.transpose(0, 1, 3, 2).reshape(g * 512, n)
def pack4(w):
    words, scales = pack_weight(w, "e2m1")
    return words.reshape(words.shape[0], 128, -1), scales


def unpack4(words, scales):
    return unpack_weight(words.reshape(words.shape[0], 128, -1, 2), scales, "e2m1")


def planes(Y):
    n, m = Y.shape
    b = f64(bf(Y)).reshape(n // 32, 32, m)
    amax = np.abs(b).max(1)
    byte = np.clip(np.where(amax > 0, np.frexp(amax)[1] - 1 + 127 - 7, 1), 1, 254)
    codes = (b * np.exp2(127.0 - byte)[:, None, :]).reshape(n, m).astype(np.float32).astype(ml_dtypes.float8_e4m3fn).view(np.uint8)
    words = codes.reshape(n // 512, 128, 4, m).transpose(0, 1, 3, 2)
    return np.ascontiguousarray(words), np.ascontiguousarray(byte.astype(np.uint8).reshape(n // 512, 16, m))


M, VA, VB, D = 1024, 1024, 2048, 1536


def setup_inputs():
    rn = np.random.randn
    s = mx_kscale(VA)
    t = mx_kscale(VB)
    wb = 1.5 * rn(VB, D) / np.sqrt(VB) / t[:, None]
    wb_words, wb_scales = pack4(wb)
    return {
        "grad_a": bf(rn(M, VA) * s[None, :]),
        "w_a": bf(rn(VA, D) / np.sqrt(VA) / s[:, None]),
        "resid_b": bf(1.2 * rn(M, VB)),
        "target_weight": bf(np.exp(0.3 * rn(VB)) * t),
        "wb_words": wb_words,
        "wb_scales": wb_scales,
        "example_weight": bf(np.exp(0.3 * rn(M))),
        "gamma": bf(np.exp(0.8 * rn(D))),
    }

def reference(grad_a, w_a, resid_b, target_weight, wb_words, wb_scales, example_weight, gamma):
    grad_b = np.tanh(f64(resid_b)) * f64(target_weight)[None, :]
    ga = mxq(f64(grad_a), 1, "e4m3")
    wa = mxq(f64(w_a), 0, "e4m3")
    gb = mxq(grad_b, 1, "e4m3")
    wb = unpack4(wb_words, wb_scales)
    de = (ga @ wa) + (gb @ wb)
    y = de * f64(example_weight)[:, None] * f64(gamma)[None, :]
    Y = y.reshape(M, D).T
    words, scales = planes(Y)
    return y, words, scales

@@ -1,0 +1,479 @@
+from contextlib import ExitStack
+
+import concourse.mybir as mybir
+from concourse.masks import make_identity
+
+M, VA, VB, D = 1024, 1024, 2048, 1536
+FLOPS = 2 * M * D * (VA + VB)
+
+F32 = mybir.dt.float32
+BF16 = mybir.dt.bfloat16
+I32 = mybir.dt.int32
+U32 = mybir.dt.uint32
+U8 = mybir.dt.uint8
+FP8X4 = mybir.dt.float8_e4m3fn_x4
+FP4X4 = mybir.dt.float4_e2m1fn_x4
+MULT = mybir.AluOpType.mult
+TANH = mybir.ActivationFunctionType.Tanh
+
+P = 128
+PACK = 4
+K_PASS = P * PACK
+N_TILE = 512
+M_TILES = M // P
+N_TILES = D // N_TILE
+A_PASSES = VA // K_PASS
+B_PASSES = VB // K_PASS
+JOB_K = 2 * K_PASS
+ACT_COLS = (256, 256, 256, 256, 128, 128)
+CAST_ACT = (1, 0)
+SORT_FROM = 5
+LAG = 4
+PAIRS = (0, 0, 0, 0, 1, 1, 1, 2, 2, 2, 2, 2)
+W_ROUND = (3, 3)
+
+
+def tile_two_loss_embedding_gradient_g5_kernel(
+    tc, grad_a, w_a, resid_b, target_weight, wb_words, wb_scales, example_weight, gamma, out_0, out_1, out_2
+):
+    nc = tc.nc
+    with ExitStack() as ctx:
+        keep = ctx.enter_context(tc.tile_pool(name="keep", bufs=1))
+        work = ctx.enter_context(tc.tile_pool(name="work", bufs=3))
+        psum = ctx.enter_context(tc.psum_pool(name="psum", bufs=1))
+        ctx.enter_context(tc.manual_schedule())
+
+        ident = keep.tile([P, P], F32, name="ident")
+        make_identity(nc, ident[:])
+
+        wb_sc = keep.tile([P, B_PASSES, D], U8, name="wb_sc", align_bytes=64)
+        nc.vector.memset(wb_sc[:].bitcast(I32), 0)
+
+        rows = {}
+        wa_raw = {}
+        wb_codes = {}
+
+        def load_rows(m, j):
+            src = resid_b[:, j * JOB_K : (j + 1) * JOB_K] if j < 2 else grad_a
+            t = work.tile([P, JOB_K], BF16, name="rows", align_bytes=64, bufs=15)
+            nc.sync.dma_start(out=t[:], in_=src[m * P : (m + 1) * P, :])
+            rows[m, j] = t
+
+        def load_wa(n, g):
+            t = keep.tile([P, PACK, N_TILE], BF16, name="wa_raw%d_%d" % (n, g), align_bytes=64)
+            src = w_a[g * K_PASS : (g + 1) * K_PASS, n * N_TILE : (n + 1) * N_TILE]
+            nc.sync.dma_start(out=t[:], in_=src.rearrange("(p t) c -> p t c", t=PACK))
+            wa_raw[n, g] = t
+
+        def load_wb(n):
+            t = keep.tile([P, B_PASSES, 2 * N_TILE], U8, name="wb_codes%d" % n, align_bytes=64)
+            src = wb_words[:, :, 2 * n * N_TILE : 2 * (n + 1) * N_TILE]
+            nc.sync.dma_start(out=t[:].bitcast(I32), in_=src.rearrange("g p b -> p g b").bitcast(I32))
+            wb_codes[n] = t
+
+        tw = keep.tile([P, B_PASSES, PACK], BF16, name="tw")
+        gam_col = keep.tile([P, N_TILES, PACK], BF16, name="gam_col")
+        ew = keep.tile([P, M_TILES, 2], BF16, name="ew")
+
+        def load_small(name):
+            if name == "tw":
+                nc.sync.dma_start(out=tw[:], in_=target_weight.rearrange("(g p t) -> p g t", p=P, t=PACK))
+            if name == "gamma":
+                nc.sync.dma_start(out=gam_col[:], in_=gamma.rearrange("(g p t) -> p g t", p=P, t=PACK))
+            if name == "ew":
+                with nc.allow_non_contiguous_dma(reason="one example weight to a partition"):
+                    nc.sync.dma_start(out=ew[:, :, 0:1], in_=example_weight.rearrange("(j p o) -> p j o", p=P, o=1))
+
+        load_rows(0, 0)
+        load_rows(0, 1)
+        load_small("tw")
+        for q in range(4):
+            nc.sync.dma_start(
+                out=wb_sc[32 * q : 32 * q + 4, :, :].bitcast(I32),
+                in_=wb_scales[:, 4 * q : 4 * q + 4, :].rearrange("g r n -> r g n").bitcast(I32),
+            )
+        load_rows(1, 0)
+        load_wb(0)
+        load_rows(1, 1)
+        load_wb(1)
+        load_rows(2, 0)
+        load_wa(0, 0)
+        load_rows(2, 1)
+        load_rows(0, 2)
+        load_wa(0, 1)
+        load_rows(1, 2)
+        load_small("gamma")
+        load_small("ew")
+        load_wa(1, 0)
+        load_wa(1, 1)
+        load_rows(3, 0)
+        load_rows(3, 1)
+        load_rows(2, 2)
+        load_rows(3, 2)
+        for j in range(3):
+            load_rows(4, j)
+        load_wa(2, 0)
+        load_wa(2, 1)
+        load_wb(2)
+
+        banks = {}
+        tanhs = {}
+        groupeds = {}
+        act_codes = {}
+        wa_codes = {}
+        gam_row = {}
+        accs = {}
+        y_tiles = {}
+        roundeds = {}
+        turneds = {}
+        gam_f32 = keep.tile([P, N_TILES, PACK], F32, name="gam_f32")
+
+        sorteds = {}
+
+        def in_sort(m, j):
+            srt = work.tile([P, 2, 2, P], F32, name="srt", bufs=4)
+            nc.scalar.copy(out=srt[:], in_=rows[m, j][:].bitcast(F32).rearrange("p (g c u) -> p g u c", g=2, u=2))
+            sorteds[m, j] = srt
+
+        def in_turn(m, j):
+            bank = psum.tile([P, 2, 2, P], F32, name="bank", bufs=8)
+            banks[m, j] = bank
+            for u in range(2):
+                for g in range(2):
+                    if (m, j) in sorteds:
+                        src = sorteds[m, j][:, g, u, :]
+                    else:
+                        src = rows[m, j][:].bitcast(F32)[:, 256 * g + u : 256 * (g + 1) : 2]
+                    nc.tensor.transpose(bank[:, u, g, :], src, ident[:])
+
+        def in_read(m, j):
+            bank = banks[m, j]
+            if j < 2:
+                th = work.tile([P, JOB_K], F32, name="th")
+                nc.scalar.activation(
+                    out=th[:].rearrange("p (c u e) -> p c u e", u=2, e=2),
+                    in_=bank[:].rearrange("p u g r -> p (u g r)").bitcast(BF16).rearrange("p (u c e) -> p c u e", u=2, e=2),
+                    func=TANH,
+                )
+                tanhs[m, j] = th
+            else:
+                grouped = work.tile([P, JOB_K], BF16, name="grouped_a", align_bytes=64)
+                nc.scalar.copy(
+                    out=grouped[:].bitcast(F32).rearrange("p (c u) -> p c u", u=2),
+                    in_=bank[:].rearrange("p u g r -> p (g r) u"),
+                )
+                groupeds[m, j] = grouped
+
+        def in_weigh(m, j):
+            grouped = work.tile([P, JOB_K], BF16, name="grouped_b", align_bytes=64)
+            nc.vector.tensor_tensor(
+                out=grouped[:].rearrange("p (g r t) -> p g r t", g=2, t=PACK),
+                in0=tanhs[m, j][:].rearrange("p (g r t) -> p g r t", g=2, t=PACK),
+                in1=tw[:, 2 * j : 2 * j + 2, :].unsqueeze(2).to_broadcast([P, 2, P, PACK]),
+                op=MULT,
+            )
+            groupeds[m, j] = grouped
+
+        def in_quantize(m, j):
+            codes = keep.tile([P, 2 * P], U32, name="act_codes%d_%d" % (m, j), align_bytes=64)
+            scales = keep.tile([P, 2 * P], U8, name="act_scales%d_%d" % (m, j), align_bytes=64)
+            nc.vector.quantize_mx(out=codes[:].bitcast(FP8X4), scales=scales[:], in_=groupeds[m, j][:])
+            act_codes[m, j] = (codes, scales)
+
+        def w_views(n, g):
+            if ("w", n, g) not in groupeds:
+                groupeds["w", n, g] = work.tile([P, N_TILE, PACK], BF16, name="w_grouped", align_bytes=64, bufs=2)
+            dst = groupeds["w", n, g][:].rearrange("p (c i) t -> p c t i", i=4)
+            src = wa_raw[n, g][:].rearrange("p t (c i) -> p c t i", i=4)
+            return dst, src, ACT_COLS[2 * n + g] // 4
+
+        def w_group_scalar(n, g):
+            dst, src, cut = w_views(n, g)
+            if cut:
+                nc.scalar.copy(out=dst[:, :cut], in_=src[:, :cut])
+
+        def w_group_vector(n, g):
+            dst, src, cut = w_views(n, g)
+            if cut < N_TILE // 4:
+                nc.vector.tensor_copy(out=dst[:, cut:], in_=src[:, cut:])
+
+        def w_quantize(n, g):
+            codes = keep.tile([P, N_TILE], U32, name="wa_codes%d_%d" % (n, g), align_bytes=64)
+            scales = keep.tile([P, N_TILE], U8, name="wa_scales%d_%d" % (n, g), align_bytes=64)
+            nc.vector.quantize_mx(
+                out=codes[:].bitcast(FP8X4), scales=scales[:], in_=groupeds["w", n, g][:].rearrange("p c t -> p (c t)")
+            )
+            wa_codes[n, g] = (codes, scales)
+
+        def gamma_turn(n):
+            bank = psum.tile([P, PACK, P], F32, name="bank", bufs=8)
+            for t in range(PACK):
+                nc.tensor.transpose(bank[:, t, :], gam_f32[:, n, t : t + 1].to_broadcast([P, P]), ident[:])
+            banks["gamma", n] = bank
+
+        def gamma_read(n):
+            row = keep.tile([P, N_TILE], F32, name="gam_row%d" % n)
+            nc.scalar.copy(
+                out=row[:].rearrange("p (c t) -> p c t", t=PACK), in_=banks["gamma", n][:].rearrange("p t c -> p c t")
+            )
+            gam_row[n] = row
+
+        def multiply(m, n, passes):
+            if (m, n) not in accs:
+                accs[m, n] = psum.tile([P, N_TILE], F32, name="bank", bufs=8)
+            acc = accs[m, n]
+            for g in passes:
+                if g < B_PASSES:
+                    codes, scales = act_codes[m, g // 2]
+                    rhs = wb_codes[n][:, g, :].bitcast(FP4X4)
+                    rhs_scale = wb_sc[:, g, n * N_TILE : (n + 1) * N_TILE]
+                else:
+                    codes, scales = act_codes[m, 2]
+                    rhs = wa_codes[n, g - B_PASSES][0][:].bitcast(FP8X4)
+                    rhs_scale = wa_codes[n, g - B_PASSES][1][:]
+                cols = slice((g % 2) * P, (g % 2 + 1) * P)
+                nc.tensor.matmul_mx(
+                    out=acc[:],
+                    lhsT=codes[:, cols].bitcast(FP8X4),
+                    lhsT_scale=scales[:, cols],
+                    rhs=rhs,
+                    rhs_scale=rhs_scale,
+                    start=(g == 0),
+                    stop=(g == A_PASSES + B_PASSES - 1),
+                )
+
+        def scale_out(m, n):
+            y = work.tile([P, N_TILE], F32, name="y", bufs=20)
+            nc.vector.scalar_tensor_tensor(
+                out=y[:], in0=accs[m, n][:], scalar=ew[:, m, 0:1], in1=gam_row[n][:], op0=MULT, op1=MULT
+            )
+            nc.sync.dma_start(out=out_0[m * P : (m + 1) * P, n * N_TILE : (n + 1) * N_TILE], in_=y[:])
+            y_tiles[m, n] = y
+
+        y_codes = {}
+        for n in range(N_TILES):
+            for h in range(M_TILES // 2):
+                y_codes[n, h] = keep.tile([P, 2 * P], U32, name="y_codes%d_%d" % (n, h), align_bytes=64)
+        y_sc_first = keep.tile([P, N_TILES - 1, M], U8, name="y_sc_first", align_bytes=64)
+        y_sc_last = keep.tile([P, 1, M], U8, name="y_sc_last", align_bytes=64)
+
+        def store_scales(tile, groups):
+            for q in range(4):
+                nc.sync.dma_start(
+                    out=out_2[groups, 4 * q : 4 * q + 4, :].rearrange("g r m -> r g m").bitcast(I32),
+                    in_=tile[32 * q : 32 * q + 4, :, :].bitcast(I32),
+                )
+
+        def out_round(unit, on_scalar):
+            rounded = work.tile([P, N_TILE], BF16, name="rounded", bufs=6)
+            dst = rounded[:].rearrange("p (u c e) -> p u c e", u=2, e=2)
+            src = y_tiles[unit][:].rearrange("p (c u e) -> p u c e", u=2, e=2)
+            if on_scalar:
+                nc.scalar.copy(out=dst, in_=src)
+            else:
+                nc.vector.tensor_copy(out=dst, in_=src)
+            roundeds[unit] = rounded
+
+        def out_turn(pair):
+            bank = psum.tile([P, 2, 2, P], F32, name="bank", bufs=8)
+            for i, unit in enumerate(pair):
+                for u in range(2):
+                    words = roundeds[unit][:].bitcast(F32)
+                    nc.tensor.transpose(bank[:, i, u, :], words[:, u * P : (u + 1) * P], ident[:])
+                banks["out", unit] = bank[:, i, :, :]
+
+        def out_read(unit):
+            turned = work.tile([P, N_TILE], BF16, name="turned", align_bytes=64, bufs=6)
+            nc.scalar.copy(
+                out=turned[:].bitcast(F32).rearrange("p (r u) -> p r u", u=2),
+                in_=banks["out", unit].rearrange("p u r -> p r u"),
+            )
+            turneds[unit] = turned
+
+        def out_quantize(unit):
+            m, n = unit
+            codes = y_codes[n, m // 2]
+            if n < N_TILES - 1:
+                scales = y_sc_first[:, n, m * P : (m + 1) * P]
+            else:
+                scales = y_sc_last[:, 0, m * P : (m + 1) * P]
+            nc.vector.quantize_mx(
+                out=codes[:, (m % 2) * P : (m % 2 + 1) * P].bitcast(FP8X4), scales=scales, in_=turneds[unit][:]
+            )
+            if m % 2 == 1:
+                cols = slice((m - 1) * P, (m + 1) * P)
+                nc.sync.dma_start(
+                    out=out_1[n, :, cols, :].rearrange("p m t -> p (m t)").bitcast(I32), in_=codes[:].bitcast(I32)
+                )
+            if unit == (M_TILES - 1, N_TILES - 2):
+                store_scales(y_sc_first, slice(0, N_TILES - 1))
+            if unit == (M_TILES - 1, N_TILES - 1):
+                store_scales(y_sc_last, slice(N_TILES - 1, N_TILES))
+
+        b_passes = range(B_PASSES)
+        a_passes = range(B_PASSES, B_PASSES + A_PASSES)
+        pending = []
+
+        def take_pairs(count):
+            pairs = []
+            for i in range(count):
+                pair = pending[:2]
+                if pair:
+                    pairs.append(pair)
+                    for unit in pair:
+                        pending.remove(unit)
+            return pairs
+
+        def scale(unit):
+            scale_out(*unit)
+            pending.append(unit)
+
+        def turn_read(m, j):
+            in_turn(m, j)
+            in_read(m, j)
+
+        turn_read(0, 0)
+        turn_read(0, 1)
+        in_weigh(0, 0)
+        in_weigh(0, 1)
+        in_quantize(0, 0)
+        turn_read(1, 0)
+        turn_read(1, 1)
+        in_quantize(0, 1)
+        in_weigh(1, 0)
+        multiply(0, 0, b_passes)
+        for j in range(3):
+            load_rows(5, j)
+        turn_read(2, 0)
+        in_weigh(1, 1)
+        in_quantize(1, 0)
+        multiply(0, 1, b_passes)
+        w_group_scalar(0, 0)
+        w_group_vector(0, 0)
+        in_quantize(1, 1)
+        turn_read(2, 1)
+        turn_read(0, 2)
+        in_weigh(2, 0)
+        w_quantize(0, 0)
+        multiply(1, 0, b_passes)
+        for j in range(3):
+            load_rows(6, j)
+        multiply(1, 1, b_passes)
+        w_group_scalar(0, 1)
+        w_group_vector(0, 1)
+        nc.vector.tensor_copy(out=gam_f32[:], in_=gam_col[:])
+        in_quantize(0, 2)
+        in_weigh(2, 1)
+        w_quantize(0, 1)
+        turn_read(1, 2)
+        gamma_turn(0)
+        gamma_read(0)
+        in_quantize(2, 0)
+        in_quantize(1, 2)
+        in_quantize(2, 1)
+        multiply(0, 0, a_passes)
+        multiply(1, 0, a_passes)
+        w_group_scalar(1, 0)
+        w_group_vector(1, 0)
+        scale((0, 0))
+        scale((1, 0))
+        multiply(2, 0, b_passes)
+        in_turn(3, 0)
+        in_turn(3, 1)
+        multiply(2, 1, b_passes)
+        for j in range(3):
+            load_rows(7, j)
+        w_group_scalar(1, 1)
+        w_group_vector(1, 1)
+        w_quantize(1, 0)
+        in_read(3, 0)
+        w_quantize(1, 1)
+        turn_read(2, 2)
+        gamma_turn(1)
+        gamma_read(1)
+        in_read(3, 1)
+        in_weigh(3, 0)
+        in_quantize(2, 2)
+        multiply(0, 1, a_passes)
+        multiply(1, 1, a_passes)
+        turn_read(3, 2)
+        in_weigh(3, 1)
+        in_quantize(3, 0)
+        scale((0, 1))
+        multiply(2, 0, a_passes)
+        multiply(2, 1, a_passes)
+        in_quantize(3, 1)
+        scale((1, 1))
+        in_quantize(3, 2)
+        if SORT_FROM <= 4:
+            for j in range(3):
+                in_sort(4, j)
+        left = [(2, 0), (2, 1)]
+        pairs = []
+        for m in range(3, M_TILES + LAG):
+            todo = [(m, 0), (m, 1)] if m < M_TILES else []
+            if m >= LAG:
+                todo.append((m - LAG, 2))
+            turning = m + 1 < M_TILES
+            if turning:
+                for j in range(3):
+                    in_turn(m + 1, j)
+            for pair in pairs:
+                out_turn(pair)
+            if m == LAG - 1:
+                gamma_turn(2)
+            if turning:
+                for j in range(3):
+                    in_read(m + 1, j)
+            if m == LAG - 1:
+                gamma_read(2)
+            turned_units = [unit for pair in pairs for unit in pair]
+            for unit in turned_units:
+                out_read(unit)
+            last_w = [g for g in range(A_PASSES) if m == W_ROUND[g]]
+            for g in last_w:
+                w_group_scalar(2, g)
+            for unit in left:
+                scale(unit)
+            left = []
+            for unit in todo:
+                multiply(*unit, range(A_PASSES + B_PASSES))
+            for g in last_w:
+                w_group_vector(2, g)
+            if turning:
+                in_weigh(m + 1, 0)
+                in_weigh(m + 1, 1)
+                in_quantize(m + 1, 0)
+            pairs = take_pairs(PAIRS[m])
+            if len(todo) > 1:
+                scale(todo[0])
+            if turning:
+                in_quantize(m + 1, 1)
+                in_quantize(m + 1, 2)
+            for g in last_w:
+                w_quantize(2, g)
+            for unit in turned_units:
+                out_quantize(unit)
+            if SORT_FROM <= m + 2 < M_TILES:
+                for j in range(3):
+                    in_sort(m + 2, j)
+            for pair in pairs:
+                for i, unit in enumerate(pair):
+                    out_round(unit, CAST_ACT[i])
+            for unit in todo[1:-1]:
+                scale(unit)
+            left = todo[-1:]
+        for unit in left:
+            scale(unit)
+        for i in range(2):
+            for pair in pairs:
+                out_turn(pair)
+            for pair in pairs:
+                for unit in pair:
+                    out_read(unit)
+                    out_quantize(unit)
+            pairs = take_pairs(2)
+            for pair in pairs:
+                for i, unit in enumerate(pair):
+                    out_round(unit, CAST_ACT[i])
+        assert not pending and not pairs

@@ -25,12 +25,15 @@ N_TILES = D // N_TILE
 A_PASSES = VA // K_PASS
 B_PASSES = VB // K_PASS
 JOB_K = 2 * K_PASS
-ACT_COLS = (256, 256, 256, 256, 128, 128)
-CAST_ACT = (1, 0)
-SORT_FROM = 5
+ACT_COLS = (0, 256, 512, 256, 512, 256)
+SORT_FROM = 9
+MERGE_FROM = 9
 LAG = 4
-PAIRS = (0, 0, 0, 0, 1, 1, 1, 2, 2, 2, 2, 2)
 W_ROUND = (3, 3)
+PAIRS = (0, 0, 2, 2, 4, 4, 4, 4)
+CAST_ACT = (1, 1)
+WARM = 1
+TAIL_UNITS = 2
 
 
 def tile_two_loss_embedding_gradient_g5_kernel(
@@ -46,77 +49,73 @@ def tile_two_loss_embedding_gradient_g5_kernel(
         ident = keep.tile([P, P], F32, name="ident")
         make_identity(nc, ident[:])
 
-        wb_sc = keep.tile([P, B_PASSES, D], U8, name="wb_sc", align_bytes=64)
-        nc.vector.memset(wb_sc[:].bitcast(I32), 0)
+        def new_bank(shape):
+            bank = psum.tile(shape, F32, name="bank", bufs=8)
+            return bank
 
         rows = {}
         wa_raw = {}
         wb_codes = {}
+        wb_sc = {}
 
-        def load_rows(m, j):
-            src = resid_b[:, j * JOB_K : (j + 1) * JOB_K] if j < 2 else grad_a
-            t = work.tile([P, JOB_K], BF16, name="rows", align_bytes=64, bufs=15)
-            nc.sync.dma_start(out=t[:], in_=src[m * P : (m + 1) * P, :])
-            rows[m, j] = t
+        def clear_scales(name, width):
+            plane = keep.tile([P, B_PASSES, width], U8, name=name, align_bytes=64)
+            nc.vector.memset(plane[:].bitcast(I32), 0)
+            return plane
 
-        def load_wa(n, g):
-            t = keep.tile([P, PACK, N_TILE], BF16, name="wa_raw%d_%d" % (n, g), align_bytes=64)
-            src = w_a[g * K_PASS : (g + 1) * K_PASS, n * N_TILE : (n + 1) * N_TILE]
+        def load_scales(plane, tiles):
+            cols = slice(tiles[0] * N_TILE, (tiles[-1] + 1) * N_TILE)
+            for r in range(4):
+                nc.sync.dma_start(
+                    out=plane[r:P:32, :, :].bitcast(I32),
+                    in_=wb_scales[:, r:16:4, cols].rearrange("g q n -> q g n").bitcast(I32),
+                )
+            for i, n in enumerate(tiles):
+                wb_sc[n] = plane[:, :, i * N_TILE : (i + 1) * N_TILE]
+
+        def load_resid(m, halves):
+            width = JOB_K * len(halves)
+            t = work.tile([P, width], BF16, name="resid%d" % len(halves), align_bytes=64, bufs=4)
+            nc.sync.dma_start(out=t[:], in_=resid_b[m * P : (m + 1) * P, halves[0] * JOB_K : halves[0] * JOB_K + width])
+            for i, j in enumerate(halves):
+                rows[m, j] = t[:, i * JOB_K : (i + 1) * JOB_K]
+
+        def load_grad(m):
+            t = work.tile([P, JOB_K], BF16, name="grad", align_bytes=64, bufs=5)
+            nc.sync.dma_start(out=t[:], in_=grad_a[m * P : (m + 1) * P, :])
+            rows[m, 2] = t[:]
+
+        def load_wa(tiles, g):
+            width = N_TILE * len(tiles)
+            t = keep.tile([P, PACK, width], BF16, name="wa_raw%d_%d" % (tiles[0], g), align_bytes=64)
+            src = w_a[g * K_PASS : (g + 1) * K_PASS, tiles[0] * N_TILE : tiles[0] * N_TILE + width]
             nc.sync.dma_start(out=t[:], in_=src.rearrange("(p t) c -> p t c", t=PACK))
-            wa_raw[n, g] = t
+            for i, n in enumerate(tiles):
+                wa_raw[n, g] = t[:, :, i * N_TILE : (i + 1) * N_TILE]
 
-        def load_wb(n):
-            t = keep.tile([P, B_PASSES, 2 * N_TILE], U8, name="wb_codes%d" % n, align_bytes=64)
-            src = wb_words[:, :, 2 * n * N_TILE : 2 * (n + 1) * N_TILE]
+        def load_wb(tiles, passes):
+            width = 2 * N_TILE * len(tiles)
+            t = keep.tile([P, len(passes), width], U8, name="wb_codes%d_%d" % (tiles[0], passes[0]), align_bytes=64)
+            src = wb_words[passes[0] : passes[-1] + 1, :, 2 * N_TILE * tiles[0] : 2 * N_TILE * tiles[0] + width]
             nc.sync.dma_start(out=t[:].bitcast(I32), in_=src.rearrange("g p b -> p g b").bitcast(I32))
-            wb_codes[n] = t
+            for i, n in enumerate(tiles):
+                for k, g in enumerate(passes):
+                    wb_codes[n, g] = t[:, k, 2 * N_TILE * i : 2 * N_TILE * (i + 1)]
 
         tw = keep.tile([P, B_PASSES, PACK], BF16, name="tw")
         gam_col = keep.tile([P, N_TILES, PACK], BF16, name="gam_col")
         ew = keep.tile([P, M_TILES, 2], BF16, name="ew")
 
-        def load_small(name):
-            if name == "tw":
-                nc.sync.dma_start(out=tw[:], in_=target_weight.rearrange("(g p t) -> p g t", p=P, t=PACK))
-            if name == "gamma":
-                nc.sync.dma_start(out=gam_col[:], in_=gamma.rearrange("(g p t) -> p g t", p=P, t=PACK))
-            if name == "ew":
-                with nc.allow_non_contiguous_dma(reason="one example weight to a partition"):
-                    nc.sync.dma_start(out=ew[:, :, 0:1], in_=example_weight.rearrange("(j p o) -> p j o", p=P, o=1))
+        def load_tw():
+            nc.sync.dma_start(out=tw[:], in_=target_weight.rearrange("(g p t) -> p g t", p=P, t=PACK))
 
-        load_rows(0, 0)
-        load_rows(0, 1)
-        load_small("tw")
-        for q in range(4):
-            nc.sync.dma_start(
-                out=wb_sc[32 * q : 32 * q + 4, :, :].bitcast(I32),
-                in_=wb_scales[:, 4 * q : 4 * q + 4, :].rearrange("g r n -> r g n").bitcast(I32),
-            )
-        load_rows(1, 0)
-        load_wb(0)
-        load_rows(1, 1)
-        load_wb(1)
-        load_rows(2, 0)
-        load_wa(0, 0)
-        load_rows(2, 1)
-        load_rows(0, 2)
-        load_wa(0, 1)
-        load_rows(1, 2)
-        load_small("gamma")
-        load_small("ew")
-        load_wa(1, 0)
-        load_wa(1, 1)
-        load_rows(3, 0)
-        load_rows(3, 1)
-        load_rows(2, 2)
-        load_rows(3, 2)
-        for j in range(3):
-            load_rows(4, j)
-        load_wa(2, 0)
-        load_wa(2, 1)
-        load_wb(2)
+        def load_gains():
+            nc.sync.dma_start(out=gam_col[:], in_=gamma.rearrange("(g p t) -> p g t", p=P, t=PACK))
+            with nc.allow_non_contiguous_dma(reason="one example weight to a partition"):
+                nc.sync.dma_start(out=ew[:, :, 0:1], in_=example_weight.rearrange("(j p o) -> p j o", p=P, o=1))
 
         banks = {}
+        sorteds = {}
         tanhs = {}
         groupeds = {}
         act_codes = {}
@@ -126,38 +125,59 @@ def tile_two_loss_embedding_gradient_g5_kernel(
         y_tiles = {}
         roundeds = {}
         turneds = {}
-        gam_f32 = keep.tile([P, N_TILES, PACK], F32, name="gam_f32")
 
-        sorteds = {}
+        def warm(count):
+            if WARM:
+                bank = new_bank([P, P])
+                for i in range(count):
+                    nc.tensor.matmul_mx(
+                        out=bank[:], lhsT=warm_codes[:].bitcast(FP8X4), lhsT_scale=warm_scales[:],
+                        rhs=warm_codes[:].bitcast(FP8X4), rhs_scale=warm_scales[:], start=True, stop=True,
+                    )
+
+        warm_zero = keep.tile([P, K_PASS], BF16, name="warm_zero", align_bytes=64)
+        warm_codes = keep.tile([P, P], U32, name="warm_codes", align_bytes=64)
+        warm_scales = keep.tile([P, P], U8, name="warm_scales", align_bytes=64)
+
+        def warm_setup():
+            if WARM:
+                nc.vector.memset(warm_zero[:], 0.0)
+                nc.vector.quantize_mx(out=warm_codes[:].bitcast(FP8X4), scales=warm_scales[:], in_=warm_zero[:])
 
         def in_sort(m, j):
-            srt = work.tile([P, 2, 2, P], F32, name="srt", bufs=4)
-            nc.scalar.copy(out=srt[:], in_=rows[m, j][:].bitcast(F32).rearrange("p (g c u) -> p g u c", g=2, u=2))
+            srt = work.tile([P, 2, 2, P], F32, name="srt", bufs=3)
+            nc.scalar.copy(out=srt[:], in_=rows[m, j].bitcast(F32).rearrange("p (g c u) -> p g u c", g=2, u=2))
             sorteds[m, j] = srt
 
         def in_turn(m, j):
-            bank = psum.tile([P, 2, 2, P], F32, name="bank", bufs=8)
+            bank = new_bank([P, 2, 2, P])
             banks[m, j] = bank
             for u in range(2):
                 for g in range(2):
                     if (m, j) in sorteds:
                         src = sorteds[m, j][:, g, u, :]
                     else:
-                        src = rows[m, j][:].bitcast(F32)[:, 256 * g + u : 256 * (g + 1) : 2]
+                        src = rows[m, j].bitcast(F32)[:, 256 * g + u : 256 * (g + 1) : 2]
                     nc.tensor.transpose(bank[:, u, g, :], src, ident[:])
 
         def in_read(m, j):
             bank = banks[m, j]
             if j < 2:
-                th = work.tile([P, JOB_K], F32, name="th")
+                if m < MERGE_FROM:
+                    th = work.tile([P, JOB_K], F32, name="th", bufs=2)
+                    tanhs[m, j] = th[:]
+                elif j == 0:
+                    th2 = work.tile([P, 2 * JOB_K], F32, name="th", bufs=2)
+                    tanhs[m] = th2
+                    tanhs[m, 0] = th2[:, :JOB_K]
+                    tanhs[m, 1] = th2[:, JOB_K:]
                 nc.scalar.activation(
-                    out=th[:].rearrange("p (c u e) -> p c u e", u=2, e=2),
+                    out=tanhs[m, j].rearrange("p (c u e) -> p c u e", u=2, e=2),
                     in_=bank[:].rearrange("p u g r -> p (u g r)").bitcast(BF16).rearrange("p (u c e) -> p c u e", u=2, e=2),
                     func=TANH,
                 )
-                tanhs[m, j] = th
             else:
-                grouped = work.tile([P, JOB_K], BF16, name="grouped_a", align_bytes=64)
+                grouped = work.tile([P, JOB_K], BF16, name="grouped_a", align_bytes=64, bufs=2)
                 nc.scalar.copy(
                     out=grouped[:].bitcast(F32).rearrange("p (c u) -> p c u", u=2),
                     in_=bank[:].rearrange("p u g r -> p (g r) u"),
@@ -165,26 +185,33 @@ def tile_two_loss_embedding_gradient_g5_kernel(
                 groupeds[m, j] = grouped
 
         def in_weigh(m, j):
-            grouped = work.tile([P, JOB_K], BF16, name="grouped_b", align_bytes=64)
+            if m >= MERGE_FROM and j == 0:
+                return
+            first, count, src = (2 * j, 2, tanhs[m, j]) if m < MERGE_FROM else (0, 4, tanhs[m][:])
+            grouped = work.tile([P, count * K_PASS], BF16, name="grouped_b", align_bytes=64, bufs=2)
             nc.vector.tensor_tensor(
-                out=grouped[:].rearrange("p (g r t) -> p g r t", g=2, t=PACK),
-                in0=tanhs[m, j][:].rearrange("p (g r t) -> p g r t", g=2, t=PACK),
-                in1=tw[:, 2 * j : 2 * j + 2, :].unsqueeze(2).to_broadcast([P, 2, P, PACK]),
+                out=grouped[:].rearrange("p (g r t) -> p g r t", g=count, t=PACK),
+                in0=src.rearrange("p (g r t) -> p g r t", g=count, t=PACK),
+                in1=tw[:, first : first + count, :].unsqueeze(2).to_broadcast([P, count, P, PACK]),
                 op=MULT,
             )
             groupeds[m, j] = grouped
 
         def in_quantize(m, j):
-            codes = keep.tile([P, 2 * P], U32, name="act_codes%d_%d" % (m, j), align_bytes=64)
-            scales = keep.tile([P, 2 * P], U8, name="act_scales%d_%d" % (m, j), align_bytes=64)
+            if m >= MERGE_FROM and j == 0:
+                return
+            first, count = (0, 4) if m >= MERGE_FROM and j == 1 else (2 * j, 2)
+            codes = keep.tile([P, count * P], U32, name="act_codes%d_%d" % (m, j), align_bytes=64)
+            scales = keep.tile([P, count * P], U8, name="act_scales%d_%d" % (m, j), align_bytes=64)
             nc.vector.quantize_mx(out=codes[:].bitcast(FP8X4), scales=scales[:], in_=groupeds[m, j][:])
-            act_codes[m, j] = (codes, scales)
+            for i in range(count):
+                act_codes[m, first + i] = (codes[:, i * P : (i + 1) * P], scales[:, i * P : (i + 1) * P])
 
         def w_views(n, g):
             if ("w", n, g) not in groupeds:
                 groupeds["w", n, g] = work.tile([P, N_TILE, PACK], BF16, name="w_grouped", align_bytes=64, bufs=2)
             dst = groupeds["w", n, g][:].rearrange("p (c i) t -> p c t i", i=4)
-            src = wa_raw[n, g][:].rearrange("p t (c i) -> p c t i", i=4)
+            src = wa_raw[n, g].rearrange("p t (c i) -> p c t i", i=4)
             return dst, src, ACT_COLS[2 * n + g] // 4
 
         def w_group_scalar(n, g):
@@ -205,275 +232,330 @@ def tile_two_loss_embedding_gradient_g5_kernel(
             )
             wa_codes[n, g] = (codes, scales)
 
-        def gamma_turn(n):
-            bank = psum.tile([P, PACK, P], F32, name="bank", bufs=8)
-            for t in range(PACK):
-                nc.tensor.transpose(bank[:, t, :], gam_f32[:, n, t : t + 1].to_broadcast([P, P]), ident[:])
-            banks["gamma", n] = bank
+        def gamma_spread(tiles):
+            count = len(tiles)
+            bank = new_bank([P, count, 2, P])
+            words = gam_col[:].bitcast(F32)
+            for i, n in enumerate(tiles):
+                for u in range(2):
+                    nc.tensor.transpose(bank[:, i, u, :], words[:, n, u : u + 1].to_broadcast([P, P]), ident[:])
+            banks["gamma", tiles] = bank
 
-        def gamma_read(n):
-            row = keep.tile([P, N_TILE], F32, name="gam_row%d" % n)
+        def gamma_read(tiles):
+            count = len(tiles)
+            row = keep.tile([P, count, N_TILE], BF16, name="gam_row%d" % tiles[0])
             nc.scalar.copy(
-                out=row[:].rearrange("p (c t) -> p c t", t=PACK), in_=banks["gamma", n][:].rearrange("p t c -> p c t")
+                out=row[:].bitcast(F32).rearrange("p i (c u) -> p i c u", u=2),
+                in_=banks["gamma", tiles][:].rearrange("p i u c -> p i c u"),
             )
-            gam_row[n] = row
+            for i, n in enumerate(tiles):
+                gam_row[n] = row[:, i, :]
 
         def multiply(m, n, passes):
             if (m, n) not in accs:
-                accs[m, n] = psum.tile([P, N_TILE], F32, name="bank", bufs=8)
+                accs[m, n] = new_bank([P, N_TILE])
             acc = accs[m, n]
             for g in passes:
+                codes, scales = act_codes[m, g]
                 if g < B_PASSES:
-                    codes, scales = act_codes[m, g // 2]
-                    rhs = wb_codes[n][:, g, :].bitcast(FP4X4)
-                    rhs_scale = wb_sc[:, g, n * N_TILE : (n + 1) * N_TILE]
+                    rhs = wb_codes[n, g].bitcast(FP4X4)
+                    rhs_scale = wb_sc[n][:, g, :]
                 else:
-                    codes, scales = act_codes[m, 2]
                     rhs = wa_codes[n, g - B_PASSES][0][:].bitcast(FP8X4)
                     rhs_scale = wa_codes[n, g - B_PASSES][1][:]
-                cols = slice((g % 2) * P, (g % 2 + 1) * P)
                 nc.tensor.matmul_mx(
                     out=acc[:],
-                    lhsT=codes[:, cols].bitcast(FP8X4),
-                    lhsT_scale=scales[:, cols],
+                    lhsT=codes.bitcast(FP8X4),
+                    lhsT_scale=scales,
                     rhs=rhs,
                     rhs_scale=rhs_scale,
                     start=(g == 0),
                     stop=(g == A_PASSES + B_PASSES - 1),
                 )
 
+        pending = []
+
         def scale_out(m, n):
-            y = work.tile([P, N_TILE], F32, name="y", bufs=20)
+            if m % 2 == 0:
+                y_tiles[m // 2, n] = work.tile([P, 2, N_TILE], F32, name="y", bufs=9)
+            y = y_tiles[m // 2, n][:, m % 2, :]
             nc.vector.scalar_tensor_tensor(
-                out=y[:], in0=accs[m, n][:], scalar=ew[:, m, 0:1], in1=gam_row[n][:], op0=MULT, op1=MULT
+                out=y, in0=accs[m, n][:], scalar=ew[:, m, 0:1], in1=gam_row[n], op0=MULT, op1=MULT
             )
-            nc.sync.dma_start(out=out_0[m * P : (m + 1) * P, n * N_TILE : (n + 1) * N_TILE], in_=y[:])
-            y_tiles[m, n] = y
+            nc.sync.dma_start(out=out_0[m * P : (m + 1) * P, n * N_TILE : (n + 1) * N_TILE], in_=y)
+            if (m // 2, n) == (M_TILES // 2 - 1, N_TILES - 1):
+                if m % 2 == 0:
+                    pending.append((m // 2, n, 0, 1))
+            elif m % 2 == 1:
+                pending.append((m // 2, n, 0, 2))
 
         y_codes = {}
         for n in range(N_TILES):
             for h in range(M_TILES // 2):
-                y_codes[n, h] = keep.tile([P, 2 * P], U32, name="y_codes%d_%d" % (n, h), align_bytes=64)
+                y_codes[h, n] = keep.tile([P, 2 * P], U32, name="y_codes%d_%d" % (h, n), align_bytes=64)
         y_sc_first = keep.tile([P, N_TILES - 1, M], U8, name="y_sc_first", align_bytes=64)
         y_sc_last = keep.tile([P, 1, M], U8, name="y_sc_last", align_bytes=64)
 
-        def store_scales(tile, groups):
-            for q in range(4):
+        def store_scales(plane, groups):
+            for r in range(4):
                 nc.sync.dma_start(
-                    out=out_2[groups, 4 * q : 4 * q + 4, :].rearrange("g r m -> r g m").bitcast(I32),
-                    in_=tile[32 * q : 32 * q + 4, :, :].bitcast(I32),
+                    out=out_2[groups, r:16:4, :].rearrange("g q m -> q g m").bitcast(I32),
+                    in_=plane[r:P:32, :, :].bitcast(I32),
                 )
 
-        def out_round(unit, on_scalar):
-            rounded = work.tile([P, N_TILE], BF16, name="rounded", bufs=6)
-            dst = rounded[:].rearrange("p (u c e) -> p u c e", u=2, e=2)
-            src = y_tiles[unit][:].rearrange("p (c u e) -> p u c e", u=2, e=2)
+        def out_round(job, on_scalar):
+            h, n, first, count = job
+            rounded = work.tile([P, 2, count, 2 * P], BF16, name="rounded", bufs=5)
+            dst = rounded[:].rearrange("p u i (c e) -> p u i c e", e=2)
+            src = y_tiles[h, n][:, first : first + count, :].rearrange("p i (c u e) -> p u i c e", u=2, e=2)
             if on_scalar:
                 nc.scalar.copy(out=dst, in_=src)
             else:
                 nc.vector.tensor_copy(out=dst, in_=src)
-            roundeds[unit] = rounded
+            words = rounded[:].bitcast(F32)
+            roundeds[job] = [[words[:, u, i, :] for u in range(2)] for i in range(count)]
 
-        def out_turn(pair):
-            bank = psum.tile([P, 2, 2, P], F32, name="bank", bufs=8)
-            for i, unit in enumerate(pair):
+        def out_round_last(m, n):
+            rounded = work.tile([P, N_TILE], BF16, name="rounded", bufs=5)
+            nc.vector.scalar_tensor_tensor(
+                out=rounded[:], in0=accs[m, n][:], scalar=ew[:, m, 0:1], in1=gam_row[n], op0=MULT, op1=MULT
+            )
+            job = (m // 2, n, m % 2, 1)
+            words = rounded[:].bitcast(F32)
+            roundeds[job] = [[words[:, u : 2 * P : 2] for u in range(2)]]
+            return job
+
+        def out_turn(job):
+            count = job[3]
+            bank = new_bank([P, count, 2, P])
+            for i in range(count):
                 for u in range(2):
-                    words = roundeds[unit][:].bitcast(F32)
-                    nc.tensor.transpose(bank[:, i, u, :], words[:, u * P : (u + 1) * P], ident[:])
-                banks["out", unit] = bank[:, i, :, :]
+                    nc.tensor.transpose(bank[:, i, u, :], roundeds[job][i][u], ident[:])
+            banks["out", job] = bank
 
-        def out_read(unit):
-            turned = work.tile([P, N_TILE], BF16, name="turned", align_bytes=64, bufs=6)
+        def out_read(job):
+            count = job[3]
+            turned = work.tile([P, count * N_TILE], BF16, name="turned", align_bytes=64, bufs=5)
             nc.scalar.copy(
-                out=turned[:].bitcast(F32).rearrange("p (r u) -> p r u", u=2),
-                in_=banks["out", unit].rearrange("p u r -> p r u"),
+                out=turned[:].bitcast(F32).rearrange("p (i r u) -> p i r u", i=count, u=2),
+                in_=banks["out", job][:].rearrange("p i u r -> p i r u"),
             )
-            turneds[unit] = turned
+            turneds[job] = turned
 
-        def out_quantize(unit):
-            m, n = unit
-            codes = y_codes[n, m // 2]
-            if n < N_TILES - 1:
-                scales = y_sc_first[:, n, m * P : (m + 1) * P]
-            else:
-                scales = y_sc_last[:, 0, m * P : (m + 1) * P]
+        def out_quantize(job):
+            h, n, first, count = job
+            codes = y_codes[h, n]
+            cols = slice((2 * h + first) * P, (2 * h + first + count) * P)
+            scales = y_sc_first[:, n, cols] if n < N_TILES - 1 else y_sc_last[:, 0, cols]
             nc.vector.quantize_mx(
-                out=codes[:, (m % 2) * P : (m % 2 + 1) * P].bitcast(FP8X4), scales=scales, in_=turneds[unit][:]
+                out=codes[:, first * P : (first + count) * P].bitcast(FP8X4), scales=scales, in_=turneds[job][:]
             )
-            if m % 2 == 1:
-                cols = slice((m - 1) * P, (m + 1) * P)
+            if first + count == 2:
                 nc.sync.dma_start(
-                    out=out_1[n, :, cols, :].rearrange("p m t -> p (m t)").bitcast(I32), in_=codes[:].bitcast(I32)
+                    out=out_1[n, :, 2 * h * P : (2 * h + 2) * P, :].rearrange("p m t -> p (m t)").bitcast(I32),
+                    in_=codes[:].bitcast(I32),
                 )
-            if unit == (M_TILES - 1, N_TILES - 2):
-                store_scales(y_sc_first, slice(0, N_TILES - 1))
-            if unit == (M_TILES - 1, N_TILES - 1):
-                store_scales(y_sc_last, slice(N_TILES - 1, N_TILES))
+                if (h, n) == (M_TILES // 2 - 1, N_TILES - 2):
+                    store_scales(y_sc_first, slice(0, N_TILES - 1))
+                if (h, n) == (M_TILES // 2 - 1, N_TILES - 1):
+                    store_scales(y_sc_last, slice(N_TILES - 1, N_TILES))
 
         b_passes = range(B_PASSES)
         a_passes = range(B_PASSES, B_PASSES + A_PASSES)
-        pending = []
-
-        def take_pairs(count):
-            pairs = []
-            for i in range(count):
-                pair = pending[:2]
-                if pair:
-                    pairs.append(pair)
-                    for unit in pair:
-                        pending.remove(unit)
-            return pairs
-
-        def scale(unit):
-            scale_out(*unit)
-            pending.append(unit)
 
         def turn_read(m, j):
             in_turn(m, j)
             in_read(m, j)
 
+        sc_first = clear_scales("wb_sc_first", 2 * N_TILE)
+        load_resid(0, (0,))
+        load_resid(0, (1,))
+        load_tw()
+        load_scales(sc_first, (0, 1))
+        warm_setup()
+        sc_last = clear_scales("wb_sc_last", N_TILE)
+        load_resid(1, (0,))
+        load_wb((0, 1), (0, 1))
+        load_resid(1, (1,))
+        load_wb((0, 1), (2, 3))
+        load_resid(2, (0, 1))
+        load_wa((0,), 0)
+        load_grad(0)
+        load_wa((0,), 1)
+        load_grad(1)
+        load_gains()
+        load_wa((1,), 0)
+        load_wa((1,), 1)
+        load_resid(3, (0, 1))
+        load_grad(2)
+        load_grad(3)
+        load_resid(4, (0, 1))
+        load_grad(4)
+        load_wa((2,), 0)
+        load_resid(5, (0, 1))
+
+        warm(8)
         turn_read(0, 0)
         turn_read(0, 1)
         in_weigh(0, 0)
         in_weigh(0, 1)
         in_quantize(0, 0)
+        warm(10)
         turn_read(1, 0)
+        warm(10)
         turn_read(1, 1)
         in_quantize(0, 1)
         in_weigh(1, 0)
-        multiply(0, 0, b_passes)
-        for j in range(3):
-            load_rows(5, j)
-        turn_read(2, 0)
-        in_weigh(1, 1)
         in_quantize(1, 0)
-        multiply(0, 1, b_passes)
+        in_weigh(1, 1)
+        in_quantize(1, 1)
+        for half in (b_passes[:2], b_passes[2:]):
+            multiply(0, 0, half)
+            multiply(0, 1, half)
+        turn_read(2, 0)
+        turn_read(2, 1)
         w_group_scalar(0, 0)
         w_group_vector(0, 0)
-        in_quantize(1, 1)
-        turn_read(2, 1)
-        turn_read(0, 2)
         in_weigh(2, 0)
         w_quantize(0, 0)
-        multiply(1, 0, b_passes)
-        for j in range(3):
-            load_rows(6, j)
-        multiply(1, 1, b_passes)
-        w_group_scalar(0, 1)
-        w_group_vector(0, 1)
-        nc.vector.tensor_copy(out=gam_f32[:], in_=gam_col[:])
-        in_quantize(0, 2)
-        in_weigh(2, 1)
-        w_quantize(0, 1)
-        turn_read(1, 2)
-        gamma_turn(0)
-        gamma_read(0)
         in_quantize(2, 0)
-        in_quantize(1, 2)
+        for half in (b_passes[:2], b_passes[2:]):
+            multiply(1, 0, half)
+            multiply(1, 1, half)
+        w_group_scalar(0, 1)
+        turn_read(0, 2)
+        turn_read(1, 2)
+        load_grad(5)
+        load_wa((2,), 1)
+        load_scales(sc_last, (2,))
+        load_wb((2,), (0, 1, 2, 3))
+        load_resid(6, (0, 1))
+        load_grad(6)
+        gamma_spread((0, 1))
+        gamma_read((0, 1))
+        in_weigh(2, 1)
         in_quantize(2, 1)
+        w_group_vector(0, 1)
+        for half in (b_passes[:2], b_passes[2:]):
+            multiply(2, 0, half)
+            multiply(2, 1, half)
+        in_quantize(0, 2)
+        w_quantize(0, 1)
+        in_quantize(1, 2)
         multiply(0, 0, a_passes)
         multiply(1, 0, a_passes)
         w_group_scalar(1, 0)
         w_group_vector(1, 0)
-        scale((0, 0))
-        scale((1, 0))
-        multiply(2, 0, b_passes)
-        in_turn(3, 0)
-        in_turn(3, 1)
-        multiply(2, 1, b_passes)
-        for j in range(3):
-            load_rows(7, j)
         w_group_scalar(1, 1)
         w_group_vector(1, 1)
         w_quantize(1, 0)
-        in_read(3, 0)
-        w_quantize(1, 1)
+        scale_out(0, 0)
+        scale_out(1, 0)
         turn_read(2, 2)
-        gamma_turn(1)
-        gamma_read(1)
-        in_read(3, 1)
-        in_weigh(3, 0)
+        turn_read(3, 0)
+        turn_read(3, 1)
+        load_resid(7, (0, 1))
+        load_grad(7)
+        w_quantize(1, 1)
         in_quantize(2, 2)
         multiply(0, 1, a_passes)
         multiply(1, 1, a_passes)
-        turn_read(3, 2)
-        in_weigh(3, 1)
-        in_quantize(3, 0)
-        scale((0, 1))
         multiply(2, 0, a_passes)
         multiply(2, 1, a_passes)
+        in_weigh(3, 0)
+        scale_out(0, 1)
+        in_quantize(3, 0)
+        in_weigh(3, 1)
+        turn_read(3, 2)
+        scale_out(1, 1)
         in_quantize(3, 1)
-        scale((1, 1))
+        scale_out(2, 0)
         in_quantize(3, 2)
-        if SORT_FROM <= 4:
-            for j in range(3):
-                in_sort(4, j)
-        left = [(2, 0), (2, 1)]
-        pairs = []
-        for m in range(3, M_TILES + LAG):
-            todo = [(m, 0), (m, 1)] if m < M_TILES else []
-            if m >= LAG:
-                todo.append((m - LAG, 2))
+        left = [(2, 1)]
+        rounds = []
+        for m in range(3, M_TILES):
+            rounds.append([(m, 0), (m, 1)] + ([(m - LAG, 2)] if m >= LAG else []))
+        rest = [(m, 2) for m in range(M_TILES - LAG, M_TILES)]
+        for i in range(0, len(rest), TAIL_UNITS):
+            rounds.append(rest[i : i + TAIL_UNITS])
+        rounded_jobs = []
+        read_jobs = []
+        for r, todo in enumerate(rounds):
+            m = r + 3
             turning = m + 1 < M_TILES
             if turning:
                 for j in range(3):
                     in_turn(m + 1, j)
-            for pair in pairs:
-                out_turn(pair)
+            turned_jobs = rounded_jobs
+            for job in turned_jobs:
+                out_turn(job)
             if m == LAG - 1:
-                gamma_turn(2)
+                gamma_spread((2,))
+            for unit in left:
+                scale_out(*unit)
+            rounded_jobs = pending[: PAIRS[r]]
+            for job in rounded_jobs:
+                pending.remove(job)
+            on_scalar = rounded_jobs[: len(rounded_jobs) * CAST_ACT[0] // CAST_ACT[1]]
+            if not turning:
+                for job in on_scalar:
+                    out_round(job, True)
             if turning:
                 for j in range(3):
                     in_read(m + 1, j)
             if m == LAG - 1:
-                gamma_read(2)
-            turned_units = [unit for pair in pairs for unit in pair]
-            for unit in turned_units:
-                out_read(unit)
+                gamma_read((2,))
+            for job in turned_jobs:
+                out_read(job)
+            if turning:
+                for job in on_scalar:
+                    out_round(job, True)
             last_w = [g for g in range(A_PASSES) if m == W_ROUND[g]]
             for g in last_w:
                 w_group_scalar(2, g)
-            for unit in left:
-                scale(unit)
-            left = []
+            if SORT_FROM <= m + 2 < M_TILES:
+                for j in range(3):
+                    in_sort(m + 2, j)
             for unit in todo:
                 multiply(*unit, range(A_PASSES + B_PASSES))
-            for g in last_w:
-                w_group_vector(2, g)
+            for job in read_jobs:
+                out_quantize(job)
+            read_jobs = turned_jobs
             if turning:
                 in_weigh(m + 1, 0)
                 in_weigh(m + 1, 1)
                 in_quantize(m + 1, 0)
-            pairs = take_pairs(PAIRS[m])
+            for job in rounded_jobs:
+                if job not in on_scalar:
+                    out_round(job, False)
             if len(todo) > 1:
-                scale(todo[0])
+                scale_out(*todo[0])
+            if not turning:
+                for job in pending[: PAIRS[r] - len(rounded_jobs)]:
+                    pending.remove(job)
+                    rounded_jobs.append(job)
+                    out_round(job, True)
             if turning:
                 in_quantize(m + 1, 1)
                 in_quantize(m + 1, 2)
             for g in last_w:
-                w_quantize(2, g)
-            for unit in turned_units:
-                out_quantize(unit)
-            if SORT_FROM <= m + 2 < M_TILES:
-                for j in range(3):
-                    in_sort(m + 2, j)
-            for pair in pairs:
-                for i, unit in enumerate(pair):
-                    out_round(unit, CAST_ACT[i])
+                w_group_vector(2, g)
+            if not turning:
+                for job in read_jobs:
+                    out_quantize(job)
+                read_jobs = []
             for unit in todo[1:-1]:
-                scale(unit)
+                scale_out(*unit)
+            for g in last_w:
+                w_quantize(2, g)
             left = todo[-1:]
-        for unit in left:
-            scale(unit)
-        for i in range(2):
-            for pair in pairs:
-                out_turn(pair)
-            for pair in pairs:
-                for unit in pair:
-                    out_read(unit)
-                    out_quantize(unit)
-            pairs = take_pairs(2)
-            for pair in pairs:
-                for i, unit in enumerate(pair):
-                    out_round(unit, CAST_ACT[i])
-        assert not pending and not pairs
+        for job in pending:
+            out_round(job, True)
+        for job in read_jobs:
+            out_quantize(job)
+        last = out_round_last(*left[0])
+        scale_out(*left[0])
+        for job in rounded_jobs + pending + [last]:
+            out_turn(job)
+            out_read(job)
+            out_quantize(job)

@@ -25,15 +25,15 @@ N_TILES = D // N_TILE
 A_PASSES = VA // K_PASS
 B_PASSES = VB // K_PASS
 JOB_K = 2 * K_PASS
-ACT_COLS = (0, 256, 512, 256, 512, 256)
-SORT_FROM = 9
+ACT_COLS = (256, 256, 512, 256, 512, 512)
+SORT_FROM = 6
 MERGE_FROM = 9
 LAG = 4
 W_ROUND = (3, 3)
-PAIRS = (0, 0, 2, 2, 4, 4, 4, 4)
-CAST_ACT = (1, 1)
+PAIRS = (0, 0, 1, 1, 4, 4, 4)
+CAST_ACT = (1, 2)
 WARM = 1
-TAIL_UNITS = 2
+TAIL_UNITS = (2, 2)
 
 
 def tile_two_loss_embedding_gradient_g5_kernel(
@@ -46,8 +46,14 @@ def tile_two_loss_embedding_gradient_g5_kernel(
         psum = ctx.enter_context(tc.psum_pool(name="psum", bufs=1))
         ctx.enter_context(tc.manual_schedule())
 
+        warm_zero = keep.tile([P, K_PASS], BF16, name="warm_zero", align_bytes=64)
+        nc.gpsimd.memset(warm_zero[:], 0.0)
+        vecs = keep.tile([P, K_PASS], BF16, name="vecs")
+        nc.gpsimd.memset(vecs[:], 0.0)
         ident = keep.tile([P, P], F32, name="ident")
         make_identity(nc, ident[:])
+        gains = keep.tile([P, K_PASS], BF16, name="gains")
+        nc.gpsimd.memset(gains[:], 0.0)
 
         def new_bank(shape):
             bank = psum.tile(shape, F32, name="bank", bufs=8)
@@ -104,15 +110,37 @@ def tile_two_loss_embedding_gradient_g5_kernel(
 
         tw = keep.tile([P, B_PASSES, PACK], BF16, name="tw")
         gam_col = keep.tile([P, N_TILES, PACK], BF16, name="gam_col")
-        ew = keep.tile([P, M_TILES, 2], BF16, name="ew")
+        ew_rows = keep.tile([P, P], F32, name="ew_rows")
+        ew = keep.tile([P, M_TILES], F32, name="ew")
+        gam_at, ew_at = 0, 8
 
         def load_tw():
-            nc.sync.dma_start(out=tw[:], in_=target_weight.rearrange("(g p t) -> p g t", p=P, t=PACK))
+            nc.sync.dma_start(out=vecs[0:B_PASSES, :], in_=target_weight.rearrange("(g k) -> g k", k=K_PASS))
 
         def load_gains():
-            nc.sync.dma_start(out=gam_col[:], in_=gamma.rearrange("(g p t) -> p g t", p=P, t=PACK))
-            with nc.allow_non_contiguous_dma(reason="one example weight to a partition"):
-                nc.sync.dma_start(out=ew[:, :, 0:1], in_=example_weight.rearrange("(j p o) -> p j o", p=P, o=1))
+            nc.sync.dma_start(out=gains[gam_at : gam_at + N_TILES, :], in_=gamma.rearrange("(g k) -> g k", k=K_PASS))
+            nc.sync.dma_start(out=gains[ew_at : ew_at + M_TILES, 0:P], in_=example_weight.rearrange("(j p) -> j p", p=P))
+
+        def turn_vecs(bank, src):
+            for u in range(2):
+                nc.tensor.transpose(bank[:, u, :], src[:].bitcast(F32)[:, u : 2 * P : 2], ident[:])
+
+        def turn_tw():
+            bank = new_bank([P, 2, P])
+            turn_vecs(bank, vecs)
+            nc.vector.tensor_copy(out=tw[:].bitcast(F32), in_=bank[:, :, 0:B_PASSES].rearrange("p u g -> p g u"))
+
+        def widen_ew():
+            nc.vector.tensor_copy(out=ew_rows[:], in_=gains[:, 0:P])
+
+        def turn_gains():
+            bank = new_bank([P, 3, P])
+            turn_vecs(bank, gains)
+            nc.tensor.transpose(bank[:, 2, :], ew_rows[:], ident[:])
+            nc.vector.tensor_copy(
+                out=gam_col[:].bitcast(F32), in_=bank[:, 0:2, gam_at : gam_at + N_TILES].rearrange("p u g -> p g u")
+            )
+            nc.vector.tensor_copy(out=ew[:], in_=bank[:, 2, ew_at : ew_at + M_TILES])
 
         banks = {}
         sorteds = {}
@@ -135,13 +163,11 @@ def tile_two_loss_embedding_gradient_g5_kernel(
                         rhs=warm_codes[:].bitcast(FP8X4), rhs_scale=warm_scales[:], start=True, stop=True,
                     )
 
-        warm_zero = keep.tile([P, K_PASS], BF16, name="warm_zero", align_bytes=64)
         warm_codes = keep.tile([P, P], U32, name="warm_codes", align_bytes=64)
         warm_scales = keep.tile([P, P], U8, name="warm_scales", align_bytes=64)
 
         def warm_setup():
             if WARM:
-                nc.vector.memset(warm_zero[:], 0.0)
                 nc.vector.quantize_mx(out=warm_codes[:].bitcast(FP8X4), scales=warm_scales[:], in_=warm_zero[:])
 
         def in_sort(m, j):
@@ -177,7 +203,7 @@ def tile_two_loss_embedding_gradient_g5_kernel(
                     func=TANH,
                 )
             else:
-                grouped = work.tile([P, JOB_K], BF16, name="grouped_a", align_bytes=64, bufs=2)
+                grouped = work.tile([P, JOB_K], BF16, name="grouped_a", align_bytes=64, bufs=3)
                 nc.scalar.copy(
                     out=grouped[:].bitcast(F32).rearrange("p (c u) -> p c u", u=2),
                     in_=bank[:].rearrange("p u g r -> p (g r) u"),
@@ -280,7 +306,7 @@ def tile_two_loss_embedding_gradient_g5_kernel(
                 y_tiles[m // 2, n] = work.tile([P, 2, N_TILE], F32, name="y", bufs=9)
             y = y_tiles[m // 2, n][:, m % 2, :]
             nc.vector.scalar_tensor_tensor(
-                out=y, in0=accs[m, n][:], scalar=ew[:, m, 0:1], in1=gam_row[n], op0=MULT, op1=MULT
+                out=y, in0=accs[m, n][:], scalar=ew[:, m : m + 1], in1=gam_row[n], op0=MULT, op1=MULT
             )
             nc.sync.dma_start(out=out_0[m * P : (m + 1) * P, n * N_TILE : (n + 1) * N_TILE], in_=y)
             if (m // 2, n) == (M_TILES // 2 - 1, N_TILES - 1):
@@ -318,7 +344,7 @@ def tile_two_loss_embedding_gradient_g5_kernel(
         def out_round_last(m, n):
             rounded = work.tile([P, N_TILE], BF16, name="rounded", bufs=5)
             nc.vector.scalar_tensor_tensor(
-                out=rounded[:], in0=accs[m, n][:], scalar=ew[:, m, 0:1], in1=gam_row[n], op0=MULT, op1=MULT
+                out=rounded[:], in0=accs[m, n][:], scalar=ew[:, m : m + 1], in1=gam_row[n], op0=MULT, op1=MULT
             )
             job = (m // 2, n, m % 2, 1)
             words = rounded[:].bitcast(F32)
@@ -368,63 +394,67 @@ def tile_two_loss_embedding_gradient_g5_kernel(
             in_read(m, j)
 
         sc_first = clear_scales("wb_sc_first", 2 * N_TILE)
+        warm_setup()
         load_resid(0, (0,))
         load_resid(0, (1,))
         load_tw()
         load_scales(sc_first, (0, 1))
-        warm_setup()
         sc_last = clear_scales("wb_sc_last", N_TILE)
         load_resid(1, (0,))
         load_wb((0, 1), (0, 1))
         load_resid(1, (1,))
         load_wb((0, 1), (2, 3))
-        load_resid(2, (0, 1))
+        warm(13)
+        turn_read(0, 0)
+        turn_read(0, 1)
+        turn_tw()
+        load_gains()
         load_wa((0,), 0)
+        load_resid(2, (0, 1))
         load_grad(0)
         load_wa((0,), 1)
         load_grad(1)
-        load_gains()
+        load_grad(2)
         load_wa((1,), 0)
         load_wa((1,), 1)
         load_resid(3, (0, 1))
-        load_grad(2)
         load_grad(3)
         load_resid(4, (0, 1))
         load_grad(4)
         load_wa((2,), 0)
         load_resid(5, (0, 1))
-
-        warm(8)
-        turn_read(0, 0)
-        turn_read(0, 1)
         in_weigh(0, 0)
         in_weigh(0, 1)
         in_quantize(0, 0)
-        warm(10)
+        warm(5)
         turn_read(1, 0)
         warm(10)
         turn_read(1, 1)
         in_quantize(0, 1)
         in_weigh(1, 0)
+        widen_ew()
         in_quantize(1, 0)
         in_weigh(1, 1)
+        w_group_scalar(0, 0)
+        w_group_vector(0, 0)
         in_quantize(1, 1)
         for half in (b_passes[:2], b_passes[2:]):
             multiply(0, 0, half)
             multiply(0, 1, half)
+        turn_gains()
         turn_read(2, 0)
         turn_read(2, 1)
-        w_group_scalar(0, 0)
-        w_group_vector(0, 0)
-        in_weigh(2, 0)
         w_quantize(0, 0)
-        in_quantize(2, 0)
+        w_group_vector(0, 1)
+        in_weigh(2, 0)
         for half in (b_passes[:2], b_passes[2:]):
             multiply(1, 0, half)
             multiply(1, 1, half)
         w_group_scalar(0, 1)
+        in_quantize(2, 0)
         turn_read(0, 2)
         turn_read(1, 2)
+        turn_read(2, 2)
         load_grad(5)
         load_wa((2,), 1)
         load_scales(sc_last, (2,))
@@ -435,49 +465,48 @@ def tile_two_loss_embedding_gradient_g5_kernel(
         gamma_read((0, 1))
         in_weigh(2, 1)
         in_quantize(2, 1)
-        w_group_vector(0, 1)
+        w_quantize(0, 1)
         for half in (b_passes[:2], b_passes[2:]):
             multiply(2, 0, half)
             multiply(2, 1, half)
         in_quantize(0, 2)
-        w_quantize(0, 1)
         in_quantize(1, 2)
+        in_quantize(2, 2)
         multiply(0, 0, a_passes)
         multiply(1, 0, a_passes)
         w_group_scalar(1, 0)
         w_group_vector(1, 0)
         w_group_scalar(1, 1)
         w_group_vector(1, 1)
-        w_quantize(1, 0)
         scale_out(0, 0)
         scale_out(1, 0)
-        turn_read(2, 2)
+        w_quantize(1, 0)
         turn_read(3, 0)
         turn_read(3, 1)
+        turn_read(3, 2)
         load_resid(7, (0, 1))
         load_grad(7)
         w_quantize(1, 1)
-        in_quantize(2, 2)
+        multiply(2, 0, a_passes)
         multiply(0, 1, a_passes)
         multiply(1, 1, a_passes)
-        multiply(2, 0, a_passes)
         multiply(2, 1, a_passes)
         in_weigh(3, 0)
-        scale_out(0, 1)
-        in_quantize(3, 0)
         in_weigh(3, 1)
-        turn_read(3, 2)
-        scale_out(1, 1)
-        in_quantize(3, 1)
+        for j in range(3):
+            in_quantize(3, j)
         scale_out(2, 0)
-        in_quantize(3, 2)
+        scale_out(0, 1)
+        scale_out(1, 1)
         left = [(2, 1)]
         rounds = []
         for m in range(3, M_TILES):
             rounds.append([(m, 0), (m, 1)] + ([(m - LAG, 2)] if m >= LAG else []))
         rest = [(m, 2) for m in range(M_TILES - LAG, M_TILES)]
-        for i in range(0, len(rest), TAIL_UNITS):
-            rounds.append(rest[i : i + TAIL_UNITS])
+        at = 0
+        for size in TAIL_UNITS:
+            rounds.append(rest[at : at + size])
+            at = at + size
         rounded_jobs = []
         read_jobs = []
         for r, todo in enumerate(rounds):
@@ -489,21 +518,21 @@ def tile_two_loss_embedding_gradient_g5_kernel(
             turned_jobs = rounded_jobs
             for job in turned_jobs:
                 out_turn(job)
-            if m == LAG - 1:
+            if m == LAG:
                 gamma_spread((2,))
             for unit in left:
                 scale_out(*unit)
             rounded_jobs = pending[: PAIRS[r]]
             for job in rounded_jobs:
                 pending.remove(job)
-            on_scalar = rounded_jobs[: len(rounded_jobs) * CAST_ACT[0] // CAST_ACT[1]]
+            on_scalar = rounded_jobs[: len(rounded_jobs) if turning else len(rounded_jobs) * CAST_ACT[0] // CAST_ACT[1]]
             if not turning:
                 for job in on_scalar:
                     out_round(job, True)
             if turning:
                 for j in range(3):
                     in_read(m + 1, j)
-            if m == LAG - 1:
+            if m == LAG:
                 gamma_read((2,))
             for job in turned_jobs:
                 out_read(job)
@@ -528,22 +557,22 @@ def tile_two_loss_embedding_gradient_g5_kernel(
             for job in rounded_jobs:
                 if job not in on_scalar:
                     out_round(job, False)
+            if not turning:
+                for job in read_jobs:
+                    out_quantize(job)
+                read_jobs = []
             if len(todo) > 1:
                 scale_out(*todo[0])
             if not turning:
                 for job in pending[: PAIRS[r] - len(rounded_jobs)]:
                     pending.remove(job)
                     rounded_jobs.append(job)
-                    out_round(job, True)
+                    out_round(job, False)
             if turning:
                 in_quantize(m + 1, 1)
                 in_quantize(m + 1, 2)
             for g in last_w:
                 w_group_vector(2, g)
-            if not turning:
-                for job in read_jobs:
-                    out_quantize(job)
-                read_jobs = []
             for unit in todo[1:-1]:
                 scale_out(*unit)
             for g in last_w:

@@ -20,20 +20,23 @@ P = 128
 PACK = 4
 K_PASS = P * PACK
 N_TILE = 512
-M_TILES = M // P
-N_TILES = D // N_TILE
+ROW_TILES = M // P
+COL_TILES = D // N_TILE
 A_PASSES = VA // K_PASS
 B_PASSES = VB // K_PASS
-JOB_K = 2 * K_PASS
-ACT_COLS = (256, 256, 512, 256, 512, 512)
-SORT_FROM = 6
-MERGE_FROM = 9
+SLAB = 2 * K_PASS
+GRAD = 2
+SLABS = 3
+PSUM_BANKS = 8
+QUADRANT = 32
+SCALE_ROWS = K_PASS // 32
+RUN = 4
+
+HEAD_TILES = 3
 LAG = 4
-W_ROUND = (3, 3)
-PAIRS = (0, 0, 1, 1, 4, 4, 4)
-CAST_ACT = (1, 2)
-WARM = 1
-TAIL_UNITS = (2, 2)
+SORT_FROM = 6
+LATE_BATCHES = PSUM_BANKS - 3
+WARM_PASSES = 10
 
 
 def tile_two_loss_embedding_gradient_g5_kernel(
@@ -42,549 +45,522 @@ def tile_two_loss_embedding_gradient_g5_kernel(
     nc = tc.nc
     with ExitStack() as ctx:
         keep = ctx.enter_context(tc.tile_pool(name="keep", bufs=1))
-        work = ctx.enter_context(tc.tile_pool(name="work", bufs=3))
+        work = ctx.enter_context(tc.tile_pool(name="work", bufs=1))
         psum = ctx.enter_context(tc.psum_pool(name="psum", bufs=1))
         ctx.enter_context(tc.manual_schedule())
 
-        warm_zero = keep.tile([P, K_PASS], BF16, name="warm_zero", align_bytes=64)
-        nc.gpsimd.memset(warm_zero[:], 0.0)
-        vecs = keep.tile([P, K_PASS], BF16, name="vecs")
-        nc.gpsimd.memset(vecs[:], 0.0)
+        weight_rows = keep.tile([P, K_PASS], BF16, name="weight_rows")
+        nc.vector.memset(weight_rows[:].bitcast(I32), 0)
+        gain_rows = keep.tile([P, K_PASS], BF16, name="gain_rows", align_bytes=64)
+        nc.gpsimd.memset(gain_rows[:].bitcast(I32), 0)
         ident = keep.tile([P, P], F32, name="ident")
         make_identity(nc, ident[:])
-        gains = keep.tile([P, K_PASS], BF16, name="gains")
-        nc.gpsimd.memset(gains[:], 0.0)
 
         def new_bank(shape):
-            bank = psum.tile(shape, F32, name="bank", bufs=8)
+            bank = psum.tile(shape, F32, name="bank", bufs=PSUM_BANKS)
             return bank
 
-        rows = {}
-        wa_raw = {}
+        slab_rows = {}
+        wa_rows = {}
         wb_codes = {}
-        wb_sc = {}
+        wb_scale = {}
 
-        def clear_scales(name, width):
+        def clear_wb_scales(name, width):
             plane = keep.tile([P, B_PASSES, width], U8, name=name, align_bytes=64)
             nc.vector.memset(plane[:].bitcast(I32), 0)
             return plane
 
-        def load_scales(plane, tiles):
+        def load_wb_scales(plane, tiles):
             cols = slice(tiles[0] * N_TILE, (tiles[-1] + 1) * N_TILE)
             for r in range(4):
                 nc.sync.dma_start(
-                    out=plane[r:P:32, :, :].bitcast(I32),
-                    in_=wb_scales[:, r:16:4, cols].rearrange("g q n -> q g n").bitcast(I32),
+                    out=plane[r:P:QUADRANT, :, :].bitcast(I32),
+                    in_=wb_scales[:, r:SCALE_ROWS:4, cols].rearrange("g q n -> q g n").bitcast(I32),
                 )
             for i, n in enumerate(tiles):
-                wb_sc[n] = plane[:, :, i * N_TILE : (i + 1) * N_TILE]
+                wb_scale[n] = plane[:, :, i * N_TILE : (i + 1) * N_TILE]
 
         def load_resid(m, halves):
-            width = JOB_K * len(halves)
-            t = work.tile([P, width], BF16, name="resid%d" % len(halves), align_bytes=64, bufs=4)
-            nc.sync.dma_start(out=t[:], in_=resid_b[m * P : (m + 1) * P, halves[0] * JOB_K : halves[0] * JOB_K + width])
+            width = SLAB * len(halves)
+            raw = work.tile([P, width], BF16, name="resid%d" % len(halves), align_bytes=64, bufs=4)
+            first = halves[0] * SLAB
+            nc.sync.dma_start(out=raw[:], in_=resid_b[m * P : (m + 1) * P, first : first + width])
             for i, j in enumerate(halves):
-                rows[m, j] = t[:, i * JOB_K : (i + 1) * JOB_K]
+                slab_rows[m, j] = raw[:, i * SLAB : (i + 1) * SLAB]
 
         def load_grad(m):
-            t = work.tile([P, JOB_K], BF16, name="grad", align_bytes=64, bufs=5)
-            nc.sync.dma_start(out=t[:], in_=grad_a[m * P : (m + 1) * P, :])
-            rows[m, 2] = t[:]
+            raw = work.tile([P, SLAB], BF16, name="grad", align_bytes=64, bufs=5)
+            nc.sync.dma_start(out=raw[:], in_=grad_a[m * P : (m + 1) * P, :])
+            slab_rows[m, GRAD] = raw[:]
 
-        def load_wa(tiles, g):
-            width = N_TILE * len(tiles)
-            t = keep.tile([P, PACK, width], BF16, name="wa_raw%d_%d" % (tiles[0], g), align_bytes=64)
-            src = w_a[g * K_PASS : (g + 1) * K_PASS, tiles[0] * N_TILE : tiles[0] * N_TILE + width]
-            nc.sync.dma_start(out=t[:], in_=src.rearrange("(p t) c -> p t c", t=PACK))
-            for i, n in enumerate(tiles):
-                wa_raw[n, g] = t[:, :, i * N_TILE : (i + 1) * N_TILE]
+        def load_wa(n, g):
+            raw = keep.tile([P, PACK, N_TILE], BF16, name="wa_rows%d_%d" % (n, g), align_bytes=64)
+            src = w_a[g * K_PASS : (g + 1) * K_PASS, n * N_TILE : (n + 1) * N_TILE]
+            nc.sync.dma_start(out=raw[:], in_=src.rearrange("(p t) c -> p t c", t=PACK))
+            wa_rows[n, g] = raw
 
         def load_wb(tiles, passes):
             width = 2 * N_TILE * len(tiles)
-            t = keep.tile([P, len(passes), width], U8, name="wb_codes%d_%d" % (tiles[0], passes[0]), align_bytes=64)
-            src = wb_words[passes[0] : passes[-1] + 1, :, 2 * N_TILE * tiles[0] : 2 * N_TILE * tiles[0] + width]
-            nc.sync.dma_start(out=t[:].bitcast(I32), in_=src.rearrange("g p b -> p g b").bitcast(I32))
+            first = 2 * N_TILE * tiles[0]
+            raw = keep.tile([P, len(passes), width], U8, name="wb%d_%d" % (tiles[0], passes[0]), align_bytes=64)
+            src = wb_words[passes[0] : passes[-1] + 1, :, first : first + width]
+            nc.sync.dma_start(out=raw[:].bitcast(I32), in_=src.rearrange("g p b -> p g b").bitcast(I32))
             for i, n in enumerate(tiles):
-                for k, g in enumerate(passes):
-                    wb_codes[n, g] = t[:, k, 2 * N_TILE * i : 2 * N_TILE * (i + 1)]
+                for slot, g in enumerate(passes):
+                    wb_codes[n, g] = raw[:, slot, 2 * N_TILE * i : 2 * N_TILE * (i + 1)]
 
-        tw = keep.tile([P, B_PASSES, PACK], BF16, name="tw")
-        gam_col = keep.tile([P, N_TILES, PACK], BF16, name="gam_col")
-        ew_rows = keep.tile([P, P], F32, name="ew_rows")
-        ew = keep.tile([P, M_TILES], F32, name="ew")
-        gam_at, ew_at = 0, 8
+        weight_col = keep.tile([P, B_PASSES, PACK], BF16, name="weight_col")
+        gamma_col = keep.tile([P, COL_TILES, PACK], BF16, name="gamma_col")
+        example_rows = keep.tile([P, P], F32, name="example_rows")
+        example_col = keep.tile([P, ROW_TILES], F32, name="example_col")
+        example_at = 8
+        gamma_row = {}
+        banks = {}
 
-        def load_tw():
-            nc.sync.dma_start(out=vecs[0:B_PASSES, :], in_=target_weight.rearrange("(g k) -> g k", k=K_PASS))
+        def load_target_weight():
+            nc.sync.dma_start(out=weight_rows[0:B_PASSES, :], in_=target_weight.rearrange("(g k) -> g k", k=K_PASS))
 
         def load_gains():
-            nc.sync.dma_start(out=gains[gam_at : gam_at + N_TILES, :], in_=gamma.rearrange("(g k) -> g k", k=K_PASS))
-            nc.sync.dma_start(out=gains[ew_at : ew_at + M_TILES, 0:P], in_=example_weight.rearrange("(j p) -> j p", p=P))
+            nc.sync.dma_start(out=gain_rows[0:COL_TILES, :], in_=gamma.rearrange("(n k) -> n k", k=K_PASS))
+            nc.sync.dma_start(
+                out=gain_rows[example_at : example_at + ROW_TILES, 0:P],
+                in_=example_weight.rearrange("(m p) -> m p", p=P),
+            )
 
-        def turn_vecs(bank, src):
+        def turn_rows(bank, rows):
             for u in range(2):
-                nc.tensor.transpose(bank[:, u, :], src[:].bitcast(F32)[:, u : 2 * P : 2], ident[:])
+                nc.tensor.transpose(bank[:, u, :], rows[:].bitcast(F32)[:, u : 2 * P : 2], ident[:])
 
-        def turn_tw():
+        def turn_target_weight():
             bank = new_bank([P, 2, P])
-            turn_vecs(bank, vecs)
-            nc.vector.tensor_copy(out=tw[:].bitcast(F32), in_=bank[:, :, 0:B_PASSES].rearrange("p u g -> p g u"))
+            turn_rows(bank, weight_rows)
+            nc.vector.tensor_copy(
+                out=weight_col[:].bitcast(F32), in_=bank[:, :, 0:B_PASSES].rearrange("p u g -> p g u")
+            )
 
-        def widen_ew():
-            nc.vector.tensor_copy(out=ew_rows[:], in_=gains[:, 0:P])
+        def widen_example_weight():
+            nc.vector.tensor_copy(out=example_rows[:], in_=gain_rows[:, 0:P])
 
         def turn_gains():
             bank = new_bank([P, 3, P])
-            turn_vecs(bank, gains)
-            nc.tensor.transpose(bank[:, 2, :], ew_rows[:], ident[:])
+            turn_rows(bank, gain_rows)
+            nc.tensor.transpose(bank[:, 2, :], example_rows[:], ident[:])
             nc.vector.tensor_copy(
-                out=gam_col[:].bitcast(F32), in_=bank[:, 0:2, gam_at : gam_at + N_TILES].rearrange("p u g -> p g u")
+                out=gamma_col[:].bitcast(F32), in_=bank[:, 0:2, 0:COL_TILES].rearrange("p u n -> p n u")
             )
-            nc.vector.tensor_copy(out=ew[:], in_=bank[:, 2, ew_at : ew_at + M_TILES])
+            nc.vector.tensor_copy(out=example_col[:], in_=bank[:, 2, example_at : example_at + ROW_TILES])
 
-        banks = {}
-        sorteds = {}
-        tanhs = {}
-        groupeds = {}
-        act_codes = {}
-        wa_codes = {}
-        gam_row = {}
-        accs = {}
-        y_tiles = {}
-        roundeds = {}
-        turneds = {}
-
-        def warm(count):
-            if WARM:
-                bank = new_bank([P, P])
-                for i in range(count):
-                    nc.tensor.matmul_mx(
-                        out=bank[:], lhsT=warm_codes[:].bitcast(FP8X4), lhsT_scale=warm_scales[:],
-                        rhs=warm_codes[:].bitcast(FP8X4), rhs_scale=warm_scales[:], start=True, stop=True,
-                    )
-
-        warm_codes = keep.tile([P, P], U32, name="warm_codes", align_bytes=64)
-        warm_scales = keep.tile([P, P], U8, name="warm_scales", align_bytes=64)
-
-        def warm_setup():
-            if WARM:
-                nc.vector.quantize_mx(out=warm_codes[:].bitcast(FP8X4), scales=warm_scales[:], in_=warm_zero[:])
-
-        def in_sort(m, j):
-            srt = work.tile([P, 2, 2, P], F32, name="srt", bufs=3)
-            nc.scalar.copy(out=srt[:], in_=rows[m, j].bitcast(F32).rearrange("p (g c u) -> p g u c", g=2, u=2))
-            sorteds[m, j] = srt
-
-        def in_turn(m, j):
-            bank = new_bank([P, 2, 2, P])
-            banks[m, j] = bank
-            for u in range(2):
-                for g in range(2):
-                    if (m, j) in sorteds:
-                        src = sorteds[m, j][:, g, u, :]
-                    else:
-                        src = rows[m, j].bitcast(F32)[:, 256 * g + u : 256 * (g + 1) : 2]
-                    nc.tensor.transpose(bank[:, u, g, :], src, ident[:])
-
-        def in_read(m, j):
-            bank = banks[m, j]
-            if j < 2:
-                if m < MERGE_FROM:
-                    th = work.tile([P, JOB_K], F32, name="th", bufs=2)
-                    tanhs[m, j] = th[:]
-                elif j == 0:
-                    th2 = work.tile([P, 2 * JOB_K], F32, name="th", bufs=2)
-                    tanhs[m] = th2
-                    tanhs[m, 0] = th2[:, :JOB_K]
-                    tanhs[m, 1] = th2[:, JOB_K:]
-                nc.scalar.activation(
-                    out=tanhs[m, j].rearrange("p (c u e) -> p c u e", u=2, e=2),
-                    in_=bank[:].rearrange("p u g r -> p (u g r)").bitcast(BF16).rearrange("p (u c e) -> p c u e", u=2, e=2),
-                    func=TANH,
-                )
-            else:
-                grouped = work.tile([P, JOB_K], BF16, name="grouped_a", align_bytes=64, bufs=3)
-                nc.scalar.copy(
-                    out=grouped[:].bitcast(F32).rearrange("p (c u) -> p c u", u=2),
-                    in_=bank[:].rearrange("p u g r -> p (g r) u"),
-                )
-                groupeds[m, j] = grouped
-
-        def in_weigh(m, j):
-            if m >= MERGE_FROM and j == 0:
-                return
-            first, count, src = (2 * j, 2, tanhs[m, j]) if m < MERGE_FROM else (0, 4, tanhs[m][:])
-            grouped = work.tile([P, count * K_PASS], BF16, name="grouped_b", align_bytes=64, bufs=2)
-            nc.vector.tensor_tensor(
-                out=grouped[:].rearrange("p (g r t) -> p g r t", g=count, t=PACK),
-                in0=src.rearrange("p (g r t) -> p g r t", g=count, t=PACK),
-                in1=tw[:, first : first + count, :].unsqueeze(2).to_broadcast([P, count, P, PACK]),
-                op=MULT,
-            )
-            groupeds[m, j] = grouped
-
-        def in_quantize(m, j):
-            if m >= MERGE_FROM and j == 0:
-                return
-            first, count = (0, 4) if m >= MERGE_FROM and j == 1 else (2 * j, 2)
-            codes = keep.tile([P, count * P], U32, name="act_codes%d_%d" % (m, j), align_bytes=64)
-            scales = keep.tile([P, count * P], U8, name="act_scales%d_%d" % (m, j), align_bytes=64)
-            nc.vector.quantize_mx(out=codes[:].bitcast(FP8X4), scales=scales[:], in_=groupeds[m, j][:])
-            for i in range(count):
-                act_codes[m, first + i] = (codes[:, i * P : (i + 1) * P], scales[:, i * P : (i + 1) * P])
-
-        def w_views(n, g):
-            if ("w", n, g) not in groupeds:
-                groupeds["w", n, g] = work.tile([P, N_TILE, PACK], BF16, name="w_grouped", align_bytes=64, bufs=2)
-            dst = groupeds["w", n, g][:].rearrange("p (c i) t -> p c t i", i=4)
-            src = wa_raw[n, g].rearrange("p t (c i) -> p c t i", i=4)
-            return dst, src, ACT_COLS[2 * n + g] // 4
-
-        def w_group_scalar(n, g):
-            dst, src, cut = w_views(n, g)
-            if cut:
-                nc.scalar.copy(out=dst[:, :cut], in_=src[:, :cut])
-
-        def w_group_vector(n, g):
-            dst, src, cut = w_views(n, g)
-            if cut < N_TILE // 4:
-                nc.vector.tensor_copy(out=dst[:, cut:], in_=src[:, cut:])
-
-        def w_quantize(n, g):
-            codes = keep.tile([P, N_TILE], U32, name="wa_codes%d_%d" % (n, g), align_bytes=64)
-            scales = keep.tile([P, N_TILE], U8, name="wa_scales%d_%d" % (n, g), align_bytes=64)
-            nc.vector.quantize_mx(
-                out=codes[:].bitcast(FP8X4), scales=scales[:], in_=groupeds["w", n, g][:].rearrange("p c t -> p (c t)")
-            )
-            wa_codes[n, g] = (codes, scales)
-
-        def gamma_spread(tiles):
-            count = len(tiles)
-            bank = new_bank([P, count, 2, P])
-            words = gam_col[:].bitcast(F32)
+        def spread_gamma(tiles):
+            bank = new_bank([P, len(tiles), 2, P])
+            pairs = gamma_col[:].bitcast(F32)
             for i, n in enumerate(tiles):
                 for u in range(2):
-                    nc.tensor.transpose(bank[:, i, u, :], words[:, n, u : u + 1].to_broadcast([P, P]), ident[:])
+                    nc.tensor.transpose(bank[:, i, u, :], pairs[:, n, u : u + 1].to_broadcast([P, P]), ident[:])
             banks["gamma", tiles] = bank
 
-        def gamma_read(tiles):
-            count = len(tiles)
-            row = keep.tile([P, count, N_TILE], BF16, name="gam_row%d" % tiles[0])
+        def read_gamma(tiles):
+            row = keep.tile([P, len(tiles), N_TILE], BF16, name="gamma_row%d" % tiles[0])
             nc.scalar.copy(
                 out=row[:].bitcast(F32).rearrange("p i (c u) -> p i c u", u=2),
                 in_=banks["gamma", tiles][:].rearrange("p i u c -> p i c u"),
             )
             for i, n in enumerate(tiles):
-                gam_row[n] = row[:, i, :]
+                gamma_row[n] = row[:, i, :]
+
+        warm_codes = keep.tile([P, P], U32, name="warm_codes", align_bytes=64)
+        warm_scales = keep.tile([P, P], U8, name="warm_scales", align_bytes=64)
+
+        def warm_up():
+            bank = new_bank([P, P])
+            for i in range(WARM_PASSES):
+                nc.tensor.matmul_mx(
+                    out=bank[:],
+                    lhsT=warm_codes[:].bitcast(FP8X4),
+                    lhsT_scale=warm_scales[:],
+                    rhs=warm_codes[:].bitcast(FP8X4),
+                    rhs_scale=warm_scales[:],
+                    start=True,
+                    stop=True,
+                )
+
+        sorted_pairs = {}
+        tanh_of = {}
+        slab_grouped = {}
+        slab_codes = {}
+
+        def sort_slab(m, j):
+            by_u = work.tile([P, 2, 2, P], F32, name="by_u", bufs=SLABS)
+            nc.scalar.copy(out=by_u[:], in_=slab_rows[m, j].bitcast(F32).rearrange("p (g c u) -> p g u c", g=2, u=2))
+            sorted_pairs[m, j] = by_u
+
+        def turn_slab(m, j):
+            bank = new_bank([P, 2, 2, P])
+            banks[m, j] = bank
+            for u in range(2):
+                for g in range(2):
+                    if (m, j) in sorted_pairs:
+                        pairs = sorted_pairs[m, j][:, g, u, :]
+                    else:
+                        pairs = slab_rows[m, j].bitcast(F32)[:, 2 * P * g + u : 2 * P * (g + 1) : 2]
+                    nc.tensor.transpose(bank[:, u, g, :], pairs, ident[:])
+
+        def read_slab(m, j):
+            bank = banks[m, j]
+            if j == GRAD:
+                grouped = work.tile([P, SLAB], BF16, name="grouped_a", align_bytes=64, bufs=HEAD_TILES)
+                nc.scalar.copy(
+                    out=grouped[:].bitcast(F32).rearrange("p (c u) -> p c u", u=2),
+                    in_=bank[:].rearrange("p u g r -> p (g r) u"),
+                )
+                slab_grouped[m, j] = grouped
+            else:
+                tanh = work.tile([P, SLAB], F32, name="tanh", bufs=2)
+                values = bank[:].rearrange("p u g r -> p (u g r)").bitcast(BF16)
+                nc.scalar.activation(
+                    out=tanh[:].rearrange("p (c u e) -> p c u e", u=2, e=2),
+                    in_=values.rearrange("p (u c e) -> p c u e", u=2, e=2),
+                    func=TANH,
+                )
+                tanh_of[m, j] = tanh
+
+        def turn_and_read(m, j):
+            turn_slab(m, j)
+            read_slab(m, j)
+
+        def weigh_slab(m, j):
+            grouped = work.tile([P, SLAB], BF16, name="grouped_b", align_bytes=64, bufs=2)
+            nc.vector.tensor_tensor(
+                out=grouped[:].rearrange("p (g r t) -> p g r t", g=2, t=PACK),
+                in0=tanh_of[m, j][:].rearrange("p (g r t) -> p g r t", g=2, t=PACK),
+                in1=weight_col[:, 2 * j : 2 * j + 2, :].unsqueeze(2).to_broadcast([P, 2, P, PACK]),
+                op=MULT,
+            )
+            slab_grouped[m, j] = grouped
+
+        def quantize_slab(m, j):
+            codes = keep.tile([P, 2 * P], U32, name="slab_codes%d_%d" % (m, j), align_bytes=64)
+            scales = keep.tile([P, 2 * P], U8, name="slab_scales%d_%d" % (m, j), align_bytes=64)
+            nc.vector.quantize_mx(out=codes[:].bitcast(FP8X4), scales=scales[:], in_=slab_grouped[m, j][:])
+            for g in range(2):
+                slab_codes[m, 2 * j + g] = (codes[:, g * P : (g + 1) * P], scales[:, g * P : (g + 1) * P])
+
+        wa_grouped = {}
+        wa_codes = {}
+
+        def regroup_wa(engine_copy, n, g, cols):
+            if (n, g) not in wa_grouped:
+                wa_grouped[n, g] = work.tile([P, N_TILE, PACK], BF16, name="wa_grouped", align_bytes=64, bufs=2)
+            engine_copy(
+                out=wa_grouped[n, g][:, cols, :].rearrange("p (c i) t -> p c t i", i=RUN),
+                in_=wa_rows[n, g][:, :, cols].rearrange("p t (c i) -> p c t i", i=RUN),
+            )
+
+        low, high, whole = slice(0, N_TILE // 2), slice(N_TILE // 2, N_TILE), slice(0, N_TILE)
+
+        def quantize_wa(n, g):
+            codes = keep.tile([P, N_TILE], U32, name="wa_codes%d_%d" % (n, g), align_bytes=64)
+            scales = keep.tile([P, N_TILE], U8, name="wa_scales%d_%d" % (n, g), align_bytes=64)
+            nc.vector.quantize_mx(
+                out=codes[:].bitcast(FP8X4), scales=scales[:], in_=wa_grouped[n, g][:].rearrange("p c t -> p (c t)")
+            )
+            wa_codes[n, g] = (codes, scales)
+
+        sums = {}
+        y_tiles = {}
+        waiting = []
+        last_pair = (ROW_TILES // 2 - 1, COL_TILES - 1)
+        b_passes = range(B_PASSES)
+        a_passes = range(B_PASSES, B_PASSES + A_PASSES)
+        all_passes = range(B_PASSES + A_PASSES)
 
         def multiply(m, n, passes):
-            if (m, n) not in accs:
-                accs[m, n] = new_bank([P, N_TILE])
-            acc = accs[m, n]
+            if (m, n) not in sums:
+                sums[m, n] = new_bank([P, N_TILE])
             for g in passes:
-                codes, scales = act_codes[m, g]
+                codes, scales = slab_codes[m, g]
                 if g < B_PASSES:
                     rhs = wb_codes[n, g].bitcast(FP4X4)
-                    rhs_scale = wb_sc[n][:, g, :]
+                    rhs_scale = wb_scale[n][:, g, :]
                 else:
                     rhs = wa_codes[n, g - B_PASSES][0][:].bitcast(FP8X4)
                     rhs_scale = wa_codes[n, g - B_PASSES][1][:]
                 nc.tensor.matmul_mx(
-                    out=acc[:],
+                    out=sums[m, n][:],
                     lhsT=codes.bitcast(FP8X4),
                     lhsT_scale=scales,
                     rhs=rhs,
                     rhs_scale=rhs_scale,
                     start=(g == 0),
-                    stop=(g == A_PASSES + B_PASSES - 1),
+                    stop=(g == B_PASSES + A_PASSES - 1),
                 )
 
-        pending = []
+        def multiply_head_b(m):
+            for half in (b_passes[:2], b_passes[2:]):
+                multiply(m, 0, half)
+                multiply(m, 1, half)
 
-        def scale_out(m, n):
+        def scale_into(out, m, n):
+            nc.vector.scalar_tensor_tensor(
+                out=out, in0=sums[m, n][:], scalar=example_col[:, m : m + 1], in1=gamma_row[n], op0=MULT, op1=MULT
+            )
+
+        def scale_and_store(m, n):
             if m % 2 == 0:
                 y_tiles[m // 2, n] = work.tile([P, 2, N_TILE], F32, name="y", bufs=9)
             y = y_tiles[m // 2, n][:, m % 2, :]
-            nc.vector.scalar_tensor_tensor(
-                out=y, in0=accs[m, n][:], scalar=ew[:, m : m + 1], in1=gam_row[n], op0=MULT, op1=MULT
-            )
+            scale_into(y, m, n)
             nc.sync.dma_start(out=out_0[m * P : (m + 1) * P, n * N_TILE : (n + 1) * N_TILE], in_=y)
-            if (m // 2, n) == (M_TILES // 2 - 1, N_TILES - 1):
+            if (m // 2, n) == last_pair:
                 if m % 2 == 0:
-                    pending.append((m // 2, n, 0, 1))
+                    waiting.append((m // 2, n, 0, 1))
             elif m % 2 == 1:
-                pending.append((m // 2, n, 0, 2))
+                waiting.append((m // 2, n, 0, 2))
 
         y_codes = {}
-        for n in range(N_TILES):
-            for h in range(M_TILES // 2):
+        for n in range(COL_TILES):
+            for h in range(ROW_TILES // 2):
                 y_codes[h, n] = keep.tile([P, 2 * P], U32, name="y_codes%d_%d" % (h, n), align_bytes=64)
-        y_sc_first = keep.tile([P, N_TILES - 1, M], U8, name="y_sc_first", align_bytes=64)
-        y_sc_last = keep.tile([P, 1, M], U8, name="y_sc_last", align_bytes=64)
+        y_scales_first = keep.tile([P, COL_TILES - 1, M], U8, name="y_scales_first", align_bytes=64)
+        y_scales_last = keep.tile([P, 1, M], U8, name="y_scales_last", align_bytes=64)
+        rounded_pairs = {}
+        turned = {}
 
-        def store_scales(plane, groups):
+        def store_scales(plane, groups, queues):
             for r in range(4):
-                nc.sync.dma_start(
-                    out=out_2[groups, r:16:4, :].rearrange("g q m -> q g m").bitcast(I32),
-                    in_=plane[r:P:32, :, :].bitcast(I32),
+                queues[r % len(queues)].dma_start(
+                    out=out_2[groups, r:SCALE_ROWS:4, :].rearrange("g q m -> q g m").bitcast(I32),
+                    in_=plane[r:P:QUADRANT, :, :].bitcast(I32),
                 )
 
-        def out_round(job, on_scalar):
-            h, n, first, count = job
-            rounded = work.tile([P, 2, count, 2 * P], BF16, name="rounded", bufs=5)
-            dst = rounded[:].rearrange("p u i (c e) -> p u i c e", e=2)
-            src = y_tiles[h, n][:, first : first + count, :].rearrange("p i (c u e) -> p u i c e", u=2, e=2)
-            if on_scalar:
-                nc.scalar.copy(out=dst, in_=src)
-            else:
-                nc.vector.tensor_copy(out=dst, in_=src)
-            words = rounded[:].bitcast(F32)
-            roundeds[job] = [[words[:, u, i, :] for u in range(2)] for i in range(count)]
-
-        def out_round_last(m, n):
-            rounded = work.tile([P, N_TILE], BF16, name="rounded", bufs=5)
-            nc.vector.scalar_tensor_tensor(
-                out=rounded[:], in0=accs[m, n][:], scalar=ew[:, m : m + 1], in1=gam_row[n], op0=MULT, op1=MULT
+        def round_batch(engine_copy, batch):
+            h, n, first, count = batch
+            rounded = work.tile([P, 2, count, 2 * P], BF16, name="rounded", bufs=LATE_BATCHES + 1)
+            engine_copy(
+                out=rounded[:].rearrange("p u i (c e) -> p u i c e", e=2),
+                in_=y_tiles[h, n][:, first : first + count, :].rearrange("p i (c u e) -> p u i c e", u=2, e=2),
             )
-            job = (m // 2, n, m % 2, 1)
-            words = rounded[:].bitcast(F32)
-            roundeds[job] = [[words[:, u : 2 * P : 2] for u in range(2)]]
-            return job
+            pairs = rounded[:].bitcast(F32)
+            rounded_pairs[batch] = [[pairs[:, u, i, :] for u in range(2)] for i in range(count)]
 
-        def out_turn(job):
-            count = job[3]
+        def round_last_unit(m, n):
+            rounded = work.tile([P, N_TILE], BF16, name="rounded", bufs=LATE_BATCHES + 1)
+            scale_into(rounded[:], m, n)
+            batch = (m // 2, n, m % 2, 1)
+            rounded_pairs[batch] = [[rounded[:].bitcast(F32)[:, u : 2 * P : 2] for u in range(2)]]
+            return batch
+
+        def turn_batch(batch):
+            count = batch[3]
             bank = new_bank([P, count, 2, P])
             for i in range(count):
                 for u in range(2):
-                    nc.tensor.transpose(bank[:, i, u, :], roundeds[job][i][u], ident[:])
-            banks["out", job] = bank
+                    nc.tensor.transpose(bank[:, i, u, :], rounded_pairs[batch][i][u], ident[:])
+            banks[batch] = bank
 
-        def out_read(job):
-            count = job[3]
-            turned = work.tile([P, count * N_TILE], BF16, name="turned", align_bytes=64, bufs=5)
+        def read_batch(batch):
+            count = batch[3]
+            grouped = work.tile([P, count * N_TILE], BF16, name="grouped_y", align_bytes=64, bufs=LATE_BATCHES)
             nc.scalar.copy(
-                out=turned[:].bitcast(F32).rearrange("p (i r u) -> p i r u", i=count, u=2),
-                in_=banks["out", job][:].rearrange("p i u r -> p i r u"),
+                out=grouped[:].bitcast(F32).rearrange("p (i r u) -> p i r u", i=count, u=2),
+                in_=banks[batch][:].rearrange("p i u r -> p i r u"),
             )
-            turneds[job] = turned
+            turned[batch] = grouped
 
-        def out_quantize(job):
-            h, n, first, count = job
+        def quantize_batch(batch):
+            h, n, first, count = batch
             codes = y_codes[h, n]
             cols = slice((2 * h + first) * P, (2 * h + first + count) * P)
-            scales = y_sc_first[:, n, cols] if n < N_TILES - 1 else y_sc_last[:, 0, cols]
+            scales = y_scales_first[:, n, cols] if n < COL_TILES - 1 else y_scales_last[:, 0, cols]
             nc.vector.quantize_mx(
-                out=codes[:, first * P : (first + count) * P].bitcast(FP8X4), scales=scales, in_=turneds[job][:]
+                out=codes[:, first * P : (first + count) * P].bitcast(FP8X4), scales=scales, in_=turned[batch][:]
             )
             if first + count == 2:
                 nc.sync.dma_start(
                     out=out_1[n, :, 2 * h * P : (2 * h + 2) * P, :].rearrange("p m t -> p (m t)").bitcast(I32),
                     in_=codes[:].bitcast(I32),
                 )
-                if (h, n) == (M_TILES // 2 - 1, N_TILES - 2):
-                    store_scales(y_sc_first, slice(0, N_TILES - 1))
-                if (h, n) == (M_TILES // 2 - 1, N_TILES - 1):
-                    store_scales(y_sc_last, slice(N_TILES - 1, N_TILES))
+                if (h, n) == (ROW_TILES // 2 - 1, COL_TILES - 2):
+                    store_scales(y_scales_first, slice(0, COL_TILES - 1), [nc.sync])
+                if (h, n) == last_pair:
+                    store_scales(y_scales_last, slice(COL_TILES - 1, COL_TILES), [nc.sync, nc.scalar])
 
-        b_passes = range(B_PASSES)
-        a_passes = range(B_PASSES, B_PASSES + A_PASSES)
+        def take_waiting(count):
+            taken = waiting[:count]
+            for batch in taken:
+                waiting.remove(batch)
+            return taken
 
-        def turn_read(m, j):
-            in_turn(m, j)
-            in_read(m, j)
-
-        sc_first = clear_scales("wb_sc_first", 2 * N_TILE)
-        warm_setup()
+        nc.vector.quantize_mx(out=warm_codes[:].bitcast(FP8X4), scales=warm_scales[:], in_=gain_rows[:])
+        scales_first = clear_wb_scales("wb_scales_first", 2 * N_TILE)
         load_resid(0, (0,))
         load_resid(0, (1,))
-        load_tw()
-        load_scales(sc_first, (0, 1))
-        sc_last = clear_scales("wb_sc_last", N_TILE)
+        load_target_weight()
         load_resid(1, (0,))
-        load_wb((0, 1), (0, 1))
+        load_wb_scales(scales_first, (0, 1))
+        scales_last = clear_wb_scales("wb_scales_last", N_TILE)
         load_resid(1, (1,))
-        load_wb((0, 1), (2, 3))
-        warm(13)
-        turn_read(0, 0)
-        turn_read(0, 1)
-        turn_tw()
+        load_wb((0, 1), b_passes[:2])
+        load_wb((0, 1), b_passes[2:])
         load_gains()
-        load_wa((0,), 0)
+        load_wa(0, 0)
         load_resid(2, (0, 1))
         load_grad(0)
-        load_wa((0,), 1)
+        load_wa(0, 1)
         load_grad(1)
         load_grad(2)
-        load_wa((1,), 0)
-        load_wa((1,), 1)
-        load_resid(3, (0, 1))
-        load_grad(3)
-        load_resid(4, (0, 1))
-        load_grad(4)
-        load_wa((2,), 0)
+        load_wa(1, 0)
+        load_wa(1, 1)
+        for m in (3, 4):
+            load_resid(m, (0, 1))
+            load_grad(m)
+        load_wa(2, 0)
         load_resid(5, (0, 1))
-        in_weigh(0, 0)
-        in_weigh(0, 1)
-        in_quantize(0, 0)
-        warm(5)
-        turn_read(1, 0)
-        warm(10)
-        turn_read(1, 1)
-        in_quantize(0, 1)
-        in_weigh(1, 0)
-        widen_ew()
-        in_quantize(1, 0)
-        in_weigh(1, 1)
-        w_group_scalar(0, 0)
-        w_group_vector(0, 0)
-        in_quantize(1, 1)
-        for half in (b_passes[:2], b_passes[2:]):
-            multiply(0, 0, half)
-            multiply(0, 1, half)
+
+        warm_up()
+        turn_and_read(0, 0)
+        turn_and_read(0, 1)
+        turn_target_weight()
+        weigh_slab(0, 0)
+        weigh_slab(0, 1)
+        quantize_slab(0, 0)
+        turn_and_read(1, 0)
+        warm_up()
+        turn_and_read(1, 1)
+        warm_up()
+        quantize_slab(0, 1)
+        weigh_slab(1, 0)
+        widen_example_weight()
+        quantize_slab(1, 0)
+        weigh_slab(1, 1)
+        regroup_wa(nc.scalar.copy, 0, 0, low)
+        regroup_wa(nc.vector.tensor_copy, 0, 0, high)
+        quantize_slab(1, 1)
+        multiply_head_b(0)
+
         turn_gains()
-        turn_read(2, 0)
-        turn_read(2, 1)
-        w_quantize(0, 0)
-        w_group_vector(0, 1)
-        in_weigh(2, 0)
-        for half in (b_passes[:2], b_passes[2:]):
-            multiply(1, 0, half)
-            multiply(1, 1, half)
-        w_group_scalar(0, 1)
-        in_quantize(2, 0)
-        turn_read(0, 2)
-        turn_read(1, 2)
-        turn_read(2, 2)
+        turn_and_read(2, 0)
+        turn_and_read(2, 1)
+        quantize_wa(0, 0)
+        regroup_wa(nc.vector.tensor_copy, 0, 1, high)
+        weigh_slab(2, 0)
+        multiply_head_b(1)
+
+        regroup_wa(nc.scalar.copy, 0, 1, low)
+        quantize_slab(2, 0)
+        for m in range(HEAD_TILES):
+            turn_and_read(m, GRAD)
         load_grad(5)
-        load_wa((2,), 1)
-        load_scales(sc_last, (2,))
-        load_wb((2,), (0, 1, 2, 3))
+        load_wa(2, 1)
+        load_wb_scales(scales_last, (2,))
+        load_wb((2,), b_passes)
         load_resid(6, (0, 1))
         load_grad(6)
-        gamma_spread((0, 1))
-        gamma_read((0, 1))
-        in_weigh(2, 1)
-        in_quantize(2, 1)
-        w_quantize(0, 1)
-        for half in (b_passes[:2], b_passes[2:]):
-            multiply(2, 0, half)
-            multiply(2, 1, half)
-        in_quantize(0, 2)
-        in_quantize(1, 2)
-        in_quantize(2, 2)
+        spread_gamma((0, 1))
+        read_gamma((0, 1))
+        weigh_slab(2, 1)
+        quantize_slab(2, 1)
+        quantize_wa(0, 1)
+        multiply_head_b(2)
+
+        for m in range(HEAD_TILES):
+            quantize_slab(m, GRAD)
         multiply(0, 0, a_passes)
         multiply(1, 0, a_passes)
-        w_group_scalar(1, 0)
-        w_group_vector(1, 0)
-        w_group_scalar(1, 1)
-        w_group_vector(1, 1)
-        scale_out(0, 0)
-        scale_out(1, 0)
-        w_quantize(1, 0)
-        turn_read(3, 0)
-        turn_read(3, 1)
-        turn_read(3, 2)
+        regroup_wa(nc.scalar.copy, 1, 0, whole)
+        regroup_wa(nc.scalar.copy, 1, 1, low)
+        regroup_wa(nc.vector.tensor_copy, 1, 1, high)
+        scale_and_store(0, 0)
+        scale_and_store(1, 0)
+        quantize_wa(1, 0)
+        for j in range(SLABS):
+            turn_and_read(HEAD_TILES, j)
         load_resid(7, (0, 1))
         load_grad(7)
-        w_quantize(1, 1)
-        multiply(2, 0, a_passes)
-        multiply(0, 1, a_passes)
-        multiply(1, 1, a_passes)
-        multiply(2, 1, a_passes)
-        in_weigh(3, 0)
-        in_weigh(3, 1)
-        for j in range(3):
-            in_quantize(3, j)
-        scale_out(2, 0)
-        scale_out(0, 1)
-        scale_out(1, 1)
-        left = [(2, 1)]
-        rounds = []
-        for m in range(3, M_TILES):
-            rounds.append([(m, 0), (m, 1)] + ([(m - LAG, 2)] if m >= LAG else []))
-        rest = [(m, 2) for m in range(M_TILES - LAG, M_TILES)]
-        at = 0
-        for size in TAIL_UNITS:
-            rounds.append(rest[at : at + size])
-            at = at + size
-        rounded_jobs = []
-        read_jobs = []
-        for r, todo in enumerate(rounds):
-            m = r + 3
-            turning = m + 1 < M_TILES
-            if turning:
-                for j in range(3):
-                    in_turn(m + 1, j)
-            turned_jobs = rounded_jobs
-            for job in turned_jobs:
-                out_turn(job)
+        quantize_wa(1, 1)
+        unscaled = [(2, 0), (0, 1), (1, 1), (2, 1)]
+        for unit in unscaled:
+            multiply(*unit, a_passes)
+        weigh_slab(HEAD_TILES, 0)
+        weigh_slab(HEAD_TILES, 1)
+        for j in range(SLABS):
+            quantize_slab(HEAD_TILES, j)
+
+        last_col = COL_TILES - 1
+        rounded_batches = []
+        read_batches = []
+        for m in range(HEAD_TILES, ROW_TILES - 1):
+            units = [(m, 0), (m, 1)] + ([(m - LAG, last_col)] if m >= LAG else [])
+            for j in range(SLABS):
+                turn_slab(m + 1, j)
+            turned_batches = rounded_batches
+            for batch in turned_batches:
+                turn_batch(batch)
             if m == LAG:
-                gamma_spread((2,))
-            for unit in left:
-                scale_out(*unit)
-            rounded_jobs = pending[: PAIRS[r]]
-            for job in rounded_jobs:
-                pending.remove(job)
-            on_scalar = rounded_jobs[: len(rounded_jobs) if turning else len(rounded_jobs) * CAST_ACT[0] // CAST_ACT[1]]
-            if not turning:
-                for job in on_scalar:
-                    out_round(job, True)
-            if turning:
-                for j in range(3):
-                    in_read(m + 1, j)
+                spread_gamma((last_col,))
+            scale_and_store(*unscaled[0])
+            rounded_batches = take_waiting(max(0, m - LAG))
+            for j in range(SLABS):
+                read_slab(m + 1, j)
             if m == LAG:
-                gamma_read((2,))
-            for job in turned_jobs:
-                out_read(job)
-            if turning:
-                for job in on_scalar:
-                    out_round(job, True)
-            last_w = [g for g in range(A_PASSES) if m == W_ROUND[g]]
-            for g in last_w:
-                w_group_scalar(2, g)
-            if SORT_FROM <= m + 2 < M_TILES:
-                for j in range(3):
-                    in_sort(m + 2, j)
-            for unit in todo:
-                multiply(*unit, range(A_PASSES + B_PASSES))
-            for job in read_jobs:
-                out_quantize(job)
-            read_jobs = turned_jobs
-            if turning:
-                in_weigh(m + 1, 0)
-                in_weigh(m + 1, 1)
-                in_quantize(m + 1, 0)
-            for job in rounded_jobs:
-                if job not in on_scalar:
-                    out_round(job, False)
-            if not turning:
-                for job in read_jobs:
-                    out_quantize(job)
-                read_jobs = []
-            if len(todo) > 1:
-                scale_out(*todo[0])
-            if not turning:
-                for job in pending[: PAIRS[r] - len(rounded_jobs)]:
-                    pending.remove(job)
-                    rounded_jobs.append(job)
-                    out_round(job, False)
-            if turning:
-                in_quantize(m + 1, 1)
-                in_quantize(m + 1, 2)
-            for g in last_w:
-                w_group_vector(2, g)
-            for unit in todo[1:-1]:
-                scale_out(*unit)
-            for g in last_w:
-                w_quantize(2, g)
-            left = todo[-1:]
-        for job in pending:
-            out_round(job, True)
-        for job in read_jobs:
-            out_quantize(job)
-        last = out_round_last(*left[0])
-        scale_out(*left[0])
-        for job in rounded_jobs + pending + [last]:
-            out_turn(job)
-            out_read(job)
-            out_quantize(job)
+                read_gamma((last_col,))
+            for batch in turned_batches:
+                read_batch(batch)
+            for batch in rounded_batches:
+                round_batch(nc.scalar.copy, batch)
+            if m == LAG - 1:
+                for g in range(A_PASSES):
+                    regroup_wa(nc.scalar.copy, last_col, g, whole)
+            if SORT_FROM <= m + 2 < ROW_TILES:
+                for j in range(SLABS):
+                    sort_slab(m + 2, j)
+            for unit in units:
+                multiply(*unit, all_passes)
+            for batch in read_batches:
+                quantize_batch(batch)
+            read_batches = turned_batches
+            weigh_slab(m + 1, 0)
+            weigh_slab(m + 1, 1)
+            quantize_slab(m + 1, 0)
+            later = unscaled[1:] + units[:-1]
+            scale_and_store(*later[0])
+            quantize_slab(m + 1, 1)
+            quantize_slab(m + 1, GRAD)
+            for unit in later[1:]:
+                scale_and_store(*unit)
+            if m == LAG - 1:
+                for g in range(A_PASSES):
+                    quantize_wa(last_col, g)
+            unscaled = units[-1:]
+
+        m = ROW_TILES - 1
+        behind = [(row, last_col) for row in range(m - LAG, ROW_TILES)]
+        for units in ([(m, 0), (m, 1), behind[0]], behind[1:-1], behind[-1:]):
+            turned_batches = rounded_batches
+            for batch in turned_batches:
+                turn_batch(batch)
+            scale_and_store(*unscaled[0])
+            rounded_batches = take_waiting(LATE_BATCHES)
+            for batch in turned_batches:
+                read_batch(batch)
+            for unit in units:
+                multiply(*unit, all_passes)
+            for batch in read_batches:
+                quantize_batch(batch)
+            read_batches = []
+            for batch in rounded_batches:
+                round_batch(nc.vector.tensor_copy, batch)
+            for batch in turned_batches:
+                quantize_batch(batch)
+            for unit in units[:-1]:
+                scale_and_store(*unit)
+            for batch in take_waiting(LATE_BATCHES - len(rounded_batches)):
+                round_batch(nc.vector.tensor_copy, batch)
+                rounded_batches.append(batch)
+            unscaled = units[-1:]
+
+        rounded_batches.append(round_last_unit(*unscaled[0]))
+        scale_and_store(*unscaled[0])
+        for batch in rounded_batches:
+            turn_batch(batch)
+            read_batch(batch)
+            quantize_batch(batch)

from contextlib import ExitStack

import concourse.mybir as mybir
from concourse.masks import make_identity

M, VA, VB, D = 1024, 1024, 2048, 1536
FLOPS = 2 * M * D * (VA + VB)

F32 = mybir.dt.float32
BF16 = mybir.dt.bfloat16
I32 = mybir.dt.int32
U32 = mybir.dt.uint32
U8 = mybir.dt.uint8
FP8X4 = mybir.dt.float8_e4m3fn_x4
FP4X4 = mybir.dt.float4_e2m1fn_x4
MULT = mybir.AluOpType.mult
TANH = mybir.ActivationFunctionType.Tanh

P = 128
PACK = 4
K_PASS = P * PACK
N_TILE = 512
ROW_TILES = M // P
COL_TILES = D // N_TILE
A_PASSES = VA // K_PASS
B_PASSES = VB // K_PASS
SLAB = 2 * K_PASS
GRAD = 2
SLABS = 3
PSUM_BANKS = 8
QUADRANT = 32
SCALE_ROWS = K_PASS // 32
RUN = 4

HEAD_TILES = 3
LAG = 4
SORT_FROM = 6
LATE_BATCHES = PSUM_BANKS - 3
WARM_PASSES = 10


def tile_two_loss_embedding_gradient_g5_kernel(
    tc, grad_a, w_a, resid_b, target_weight, wb_words, wb_scales, example_weight, gamma, out_0, out_1, out_2
):
    nc = tc.nc
    with ExitStack() as ctx:
        keep = ctx.enter_context(tc.tile_pool(name="keep", bufs=1))
        work = ctx.enter_context(tc.tile_pool(name="work", bufs=1))
        psum = ctx.enter_context(tc.psum_pool(name="psum", bufs=1))
        ctx.enter_context(tc.manual_schedule())

        weight_rows = keep.tile([P, K_PASS], BF16, name="weight_rows")
        nc.vector.memset(weight_rows[:].bitcast(I32), 0)
        gain_rows = keep.tile([P, K_PASS], BF16, name="gain_rows", align_bytes=64)
        nc.gpsimd.memset(gain_rows[:].bitcast(I32), 0)
        ident = keep.tile([P, P], F32, name="ident")
        make_identity(nc, ident[:])

        def new_bank(shape):
            bank = psum.tile(shape, F32, name="bank", bufs=PSUM_BANKS)
            return bank

        slab_rows = {}
        wa_rows = {}
        wb_codes = {}
        wb_scale = {}

        def clear_wb_scales(name, width):
            plane = keep.tile([P, B_PASSES, width], U8, name=name, align_bytes=64)
            nc.vector.memset(plane[:].bitcast(I32), 0)
            return plane

        def load_wb_scales(plane, tiles):
            cols = slice(tiles[0] * N_TILE, (tiles[-1] + 1) * N_TILE)
            for r in range(4):
                nc.sync.dma_start(
                    out=plane[r:P:QUADRANT, :, :].bitcast(I32),
                    in_=wb_scales[:, r:SCALE_ROWS:4, cols].rearrange("g q n -> q g n").bitcast(I32),
                )
            for i, n in enumerate(tiles):
                wb_scale[n] = plane[:, :, i * N_TILE : (i + 1) * N_TILE]

        def load_resid(m, halves):
            width = SLAB * len(halves)
            raw = work.tile([P, width], BF16, name="resid%d" % len(halves), align_bytes=64, bufs=4)
            first = halves[0] * SLAB
            nc.sync.dma_start(out=raw[:], in_=resid_b[m * P : (m + 1) * P, first : first + width])
            for i, j in enumerate(halves):
                slab_rows[m, j] = raw[:, i * SLAB : (i + 1) * SLAB]

        def load_grad(m):
            raw = work.tile([P, SLAB], BF16, name="grad", align_bytes=64, bufs=5)
            nc.sync.dma_start(out=raw[:], in_=grad_a[m * P : (m + 1) * P, :])
            slab_rows[m, GRAD] = raw[:]

        def load_wa(n, g):
            raw = keep.tile([P, PACK, N_TILE], BF16, name="wa_rows%d_%d" % (n, g), align_bytes=64)
            src = w_a[g * K_PASS : (g + 1) * K_PASS, n * N_TILE : (n + 1) * N_TILE]
            nc.sync.dma_start(out=raw[:], in_=src.rearrange("(p t) c -> p t c", t=PACK))
            wa_rows[n, g] = raw

        def load_wb(tiles, passes):
            width = 2 * N_TILE * len(tiles)
            first = 2 * N_TILE * tiles[0]
            raw = keep.tile([P, len(passes), width], U8, name="wb%d_%d" % (tiles[0], passes[0]), align_bytes=64)
            src = wb_words[passes[0] : passes[-1] + 1, :, first : first + width]
            nc.sync.dma_start(out=raw[:].bitcast(I32), in_=src.rearrange("g p b -> p g b").bitcast(I32))
            for i, n in enumerate(tiles):
                for slot, g in enumerate(passes):
                    wb_codes[n, g] = raw[:, slot, 2 * N_TILE * i : 2 * N_TILE * (i + 1)]

        weight_col = keep.tile([P, B_PASSES, PACK], BF16, name="weight_col")
        gamma_col = keep.tile([P, COL_TILES, PACK], BF16, name="gamma_col")
        example_rows = keep.tile([P, P], F32, name="example_rows")
        example_col = keep.tile([P, ROW_TILES], F32, name="example_col")
        example_at = 8
        gamma_row = {}
        banks = {}

        def load_target_weight():
            nc.sync.dma_start(out=weight_rows[0:B_PASSES, :], in_=target_weight.rearrange("(g k) -> g k", k=K_PASS))

        def load_gains():
            nc.sync.dma_start(out=gain_rows[0:COL_TILES, :], in_=gamma.rearrange("(n k) -> n k", k=K_PASS))
            nc.sync.dma_start(
                out=gain_rows[example_at : example_at + ROW_TILES, 0:P],
                in_=example_weight.rearrange("(m p) -> m p", p=P),
            )

        def turn_rows(bank, rows):
            for u in range(2):
                nc.tensor.transpose(bank[:, u, :], rows[:].bitcast(F32)[:, u : 2 * P : 2], ident[:])

        def turn_target_weight():
            bank = new_bank([P, 2, P])
            turn_rows(bank, weight_rows)
            nc.vector.tensor_copy(
                out=weight_col[:].bitcast(F32), in_=bank[:, :, 0:B_PASSES].rearrange("p u g -> p g u")
            )

        def widen_example_weight():
            nc.vector.tensor_copy(out=example_rows[:], in_=gain_rows[:, 0:P])

        def turn_gains():
            bank = new_bank([P, 3, P])
            turn_rows(bank, gain_rows)
            nc.tensor.transpose(bank[:, 2, :], example_rows[:], ident[:])
            nc.vector.tensor_copy(
                out=gamma_col[:].bitcast(F32), in_=bank[:, 0:2, 0:COL_TILES].rearrange("p u n -> p n u")
            )
            nc.vector.tensor_copy(out=example_col[:], in_=bank[:, 2, example_at : example_at + ROW_TILES])

        def spread_gamma(tiles):
            bank = new_bank([P, len(tiles), 2, P])
            pairs = gamma_col[:].bitcast(F32)
            for i, n in enumerate(tiles):
                for u in range(2):
                    nc.tensor.transpose(bank[:, i, u, :], pairs[:, n, u : u + 1].to_broadcast([P, P]), ident[:])
            banks["gamma", tiles] = bank

        def read_gamma(tiles):
            row = keep.tile([P, len(tiles), N_TILE], BF16, name="gamma_row%d" % tiles[0])
            nc.scalar.copy(
                out=row[:].bitcast(F32).rearrange("p i (c u) -> p i c u", u=2),
                in_=banks["gamma", tiles][:].rearrange("p i u c -> p i c u"),
            )
            for i, n in enumerate(tiles):
                gamma_row[n] = row[:, i, :]

        warm_codes = keep.tile([P, P], U32, name="warm_codes", align_bytes=64)
        warm_scales = keep.tile([P, P], U8, name="warm_scales", align_bytes=64)

        def warm_up():
            bank = new_bank([P, P])
            for i in range(WARM_PASSES):
                nc.tensor.matmul_mx(
                    out=bank[:],
                    lhsT=warm_codes[:].bitcast(FP8X4),
                    lhsT_scale=warm_scales[:],
                    rhs=warm_codes[:].bitcast(FP8X4),
                    rhs_scale=warm_scales[:],
                    start=True,
                    stop=True,
                )

        sorted_pairs = {}
        tanh_of = {}
        slab_grouped = {}
        slab_codes = {}

        def sort_slab(m, j):
            by_u = work.tile([P, 2, 2, P], F32, name="by_u", bufs=SLABS)
            nc.scalar.copy(out=by_u[:], in_=slab_rows[m, j].bitcast(F32).rearrange("p (g c u) -> p g u c", g=2, u=2))
            sorted_pairs[m, j] = by_u

        def turn_slab(m, j):
            bank = new_bank([P, 2, 2, P])
            banks[m, j] = bank
            for u in range(2):
                for g in range(2):
                    if (m, j) in sorted_pairs:
                        pairs = sorted_pairs[m, j][:, g, u, :]
                    else:
                        pairs = slab_rows[m, j].bitcast(F32)[:, 2 * P * g + u : 2 * P * (g + 1) : 2]
                    nc.tensor.transpose(bank[:, u, g, :], pairs, ident[:])

        def read_slab(m, j):
            bank = banks[m, j]
            if j == GRAD:
                grouped = work.tile([P, SLAB], BF16, name="grouped_a", align_bytes=64, bufs=HEAD_TILES)
                nc.scalar.copy(
                    out=grouped[:].bitcast(F32).rearrange("p (c u) -> p c u", u=2),
                    in_=bank[:].rearrange("p u g r -> p (g r) u"),
                )
                slab_grouped[m, j] = grouped
            else:
                tanh = work.tile([P, SLAB], F32, name="tanh", bufs=2)
                values = bank[:].rearrange("p u g r -> p (u g r)").bitcast(BF16)
                nc.scalar.activation(
                    out=tanh[:].rearrange("p (c u e) -> p c u e", u=2, e=2),
                    in_=values.rearrange("p (u c e) -> p c u e", u=2, e=2),
                    func=TANH,
                )
                tanh_of[m, j] = tanh

        def turn_and_read(m, j):
            turn_slab(m, j)
            read_slab(m, j)

        def weigh_slab(m, j):
            grouped = work.tile([P, SLAB], BF16, name="grouped_b", align_bytes=64, bufs=2)
            nc.vector.tensor_tensor(
                out=grouped[:].rearrange("p (g r t) -> p g r t", g=2, t=PACK),
                in0=tanh_of[m, j][:].rearrange("p (g r t) -> p g r t", g=2, t=PACK),
                in1=weight_col[:, 2 * j : 2 * j + 2, :].unsqueeze(2).to_broadcast([P, 2, P, PACK]),
                op=MULT,
            )
            slab_grouped[m, j] = grouped

        def quantize_slab(m, j):
            codes = keep.tile([P, 2 * P], U32, name="slab_codes%d_%d" % (m, j), align_bytes=64)
            scales = keep.tile([P, 2 * P], U8, name="slab_scales%d_%d" % (m, j), align_bytes=64)
            nc.vector.quantize_mx(out=codes[:].bitcast(FP8X4), scales=scales[:], in_=slab_grouped[m, j][:])
            for g in range(2):
                slab_codes[m, 2 * j + g] = (codes[:, g * P : (g + 1) * P], scales[:, g * P : (g + 1) * P])

        wa_grouped = {}
        wa_codes = {}

        def regroup_wa(engine_copy, n, g, cols):
            if (n, g) not in wa_grouped:
                wa_grouped[n, g] = work.tile([P, N_TILE, PACK], BF16, name="wa_grouped", align_bytes=64, bufs=2)
            engine_copy(
                out=wa_grouped[n, g][:, cols, :].rearrange("p (c i) t -> p c t i", i=RUN),
                in_=wa_rows[n, g][:, :, cols].rearrange("p t (c i) -> p c t i", i=RUN),
            )

        low, high, whole = slice(0, N_TILE // 2), slice(N_TILE // 2, N_TILE), slice(0, N_TILE)

        def quantize_wa(n, g):
            codes = keep.tile([P, N_TILE], U32, name="wa_codes%d_%d" % (n, g), align_bytes=64)
            scales = keep.tile([P, N_TILE], U8, name="wa_scales%d_%d" % (n, g), align_bytes=64)
            nc.vector.quantize_mx(
                out=codes[:].bitcast(FP8X4), scales=scales[:], in_=wa_grouped[n, g][:].rearrange("p c t -> p (c t)")
            )
            wa_codes[n, g] = (codes, scales)

        sums = {}
        y_tiles = {}
        waiting = []
        last_pair = (ROW_TILES // 2 - 1, COL_TILES - 1)
        b_passes = range(B_PASSES)
        a_passes = range(B_PASSES, B_PASSES + A_PASSES)
        all_passes = range(B_PASSES + A_PASSES)

        def multiply(m, n, passes):
            if (m, n) not in sums:
                sums[m, n] = new_bank([P, N_TILE])
            for g in passes:
                codes, scales = slab_codes[m, g]
                if g < B_PASSES:
                    rhs = wb_codes[n, g].bitcast(FP4X4)
                    rhs_scale = wb_scale[n][:, g, :]
                else:
                    rhs = wa_codes[n, g - B_PASSES][0][:].bitcast(FP8X4)
                    rhs_scale = wa_codes[n, g - B_PASSES][1][:]
                nc.tensor.matmul_mx(
                    out=sums[m, n][:],
                    lhsT=codes.bitcast(FP8X4),
                    lhsT_scale=scales,
                    rhs=rhs,
                    rhs_scale=rhs_scale,
                    start=(g == 0),
                    stop=(g == B_PASSES + A_PASSES - 1),
                )

        def multiply_head_b(m):
            for half in (b_passes[:2], b_passes[2:]):
                multiply(m, 0, half)
                multiply(m, 1, half)

        def scale_into(out, m, n):
            nc.vector.scalar_tensor_tensor(
                out=out, in0=sums[m, n][:], scalar=example_col[:, m : m + 1], in1=gamma_row[n], op0=MULT, op1=MULT
            )

        def scale_and_store(m, n):
            if m % 2 == 0:
                y_tiles[m // 2, n] = work.tile([P, 2, N_TILE], F32, name="y", bufs=9)
            y = y_tiles[m // 2, n][:, m % 2, :]
            scale_into(y, m, n)
            nc.sync.dma_start(out=out_0[m * P : (m + 1) * P, n * N_TILE : (n + 1) * N_TILE], in_=y)
            if (m // 2, n) == last_pair:
                if m % 2 == 0:
                    waiting.append((m // 2, n, 0, 1))
            elif m % 2 == 1:
                waiting.append((m // 2, n, 0, 2))

        y_codes = {}
        for n in range(COL_TILES):
            for h in range(ROW_TILES // 2):
                y_codes[h, n] = keep.tile([P, 2 * P], U32, name="y_codes%d_%d" % (h, n), align_bytes=64)
        y_scales_first = keep.tile([P, COL_TILES - 1, M], U8, name="y_scales_first", align_bytes=64)
        y_scales_last = keep.tile([P, 1, M], U8, name="y_scales_last", align_bytes=64)
        rounded_pairs = {}
        turned = {}

        def store_scales(plane, groups, queues):
            for r in range(4):
                queues[r % len(queues)].dma_start(
                    out=out_2[groups, r:SCALE_ROWS:4, :].rearrange("g q m -> q g m").bitcast(I32),
                    in_=plane[r:P:QUADRANT, :, :].bitcast(I32),
                )

        def round_batch(engine_copy, batch):
            h, n, first, count = batch
            rounded = work.tile([P, 2, count, 2 * P], BF16, name="rounded", bufs=LATE_BATCHES + 1)
            engine_copy(
                out=rounded[:].rearrange("p u i (c e) -> p u i c e", e=2),
                in_=y_tiles[h, n][:, first : first + count, :].rearrange("p i (c u e) -> p u i c e", u=2, e=2),
            )
            pairs = rounded[:].bitcast(F32)
            rounded_pairs[batch] = [[pairs[:, u, i, :] for u in range(2)] for i in range(count)]

        def round_last_unit(m, n):
            rounded = work.tile([P, N_TILE], BF16, name="rounded", bufs=LATE_BATCHES + 1)
            scale_into(rounded[:], m, n)
            batch = (m // 2, n, m % 2, 1)
            rounded_pairs[batch] = [[rounded[:].bitcast(F32)[:, u : 2 * P : 2] for u in range(2)]]
            return batch

        def turn_batch(batch):
            count = batch[3]
            bank = new_bank([P, count, 2, P])
            for i in range(count):
                for u in range(2):
                    nc.tensor.transpose(bank[:, i, u, :], rounded_pairs[batch][i][u], ident[:])
            banks[batch] = bank

        def read_batch(batch):
            count = batch[3]
            grouped = work.tile([P, count * N_TILE], BF16, name="grouped_y", align_bytes=64, bufs=LATE_BATCHES)
            nc.scalar.copy(
                out=grouped[:].bitcast(F32).rearrange("p (i r u) -> p i r u", i=count, u=2),
                in_=banks[batch][:].rearrange("p i u r -> p i r u"),
            )
            turned[batch] = grouped

        def quantize_batch(batch):
            h, n, first, count = batch
            codes = y_codes[h, n]
            cols = slice((2 * h + first) * P, (2 * h + first + count) * P)
            scales = y_scales_first[:, n, cols] if n < COL_TILES - 1 else y_scales_last[:, 0, cols]
            nc.vector.quantize_mx(
                out=codes[:, first * P : (first + count) * P].bitcast(FP8X4), scales=scales, in_=turned[batch][:]
            )
            if first + count == 2:
                nc.sync.dma_start(
                    out=out_1[n, :, 2 * h * P : (2 * h + 2) * P, :].rearrange("p m t -> p (m t)").bitcast(I32),
                    in_=codes[:].bitcast(I32),
                )
                if (h, n) == (ROW_TILES // 2 - 1, COL_TILES - 2):
                    store_scales(y_scales_first, slice(0, COL_TILES - 1), [nc.sync])
                if (h, n) == last_pair:
                    store_scales(y_scales_last, slice(COL_TILES - 1, COL_TILES), [nc.sync, nc.scalar])

        def take_waiting(count):
            taken = waiting[:count]
            for batch in taken:
                waiting.remove(batch)
            return taken

        nc.vector.quantize_mx(out=warm_codes[:].bitcast(FP8X4), scales=warm_scales[:], in_=gain_rows[:])
        scales_first = clear_wb_scales("wb_scales_first", 2 * N_TILE)
        load_resid(0, (0,))
        load_resid(0, (1,))
        load_target_weight()
        load_resid(1, (0,))
        load_wb_scales(scales_first, (0, 1))
        scales_last = clear_wb_scales("wb_scales_last", N_TILE)
        load_resid(1, (1,))
        load_wb((0, 1), b_passes[:2])
        load_wb((0, 1), b_passes[2:])
        load_gains()
        load_wa(0, 0)
        load_resid(2, (0, 1))
        load_grad(0)
        load_wa(0, 1)
        load_grad(1)
        load_grad(2)
        load_wa(1, 0)
        load_wa(1, 1)
        for m in (3, 4):
            load_resid(m, (0, 1))
            load_grad(m)
        load_wa(2, 0)
        load_resid(5, (0, 1))

        warm_up()
        turn_and_read(0, 0)
        turn_and_read(0, 1)
        turn_target_weight()
        weigh_slab(0, 0)
        weigh_slab(0, 1)
        quantize_slab(0, 0)
        turn_and_read(1, 0)
        warm_up()
        turn_and_read(1, 1)
        warm_up()
        quantize_slab(0, 1)
        weigh_slab(1, 0)
        widen_example_weight()
        quantize_slab(1, 0)
        weigh_slab(1, 1)
        regroup_wa(nc.scalar.copy, 0, 0, low)
        regroup_wa(nc.vector.tensor_copy, 0, 0, high)
        quantize_slab(1, 1)
        multiply_head_b(0)

        turn_gains()
        turn_and_read(2, 0)
        turn_and_read(2, 1)
        quantize_wa(0, 0)
        regroup_wa(nc.vector.tensor_copy, 0, 1, high)
        weigh_slab(2, 0)
        multiply_head_b(1)

        regroup_wa(nc.scalar.copy, 0, 1, low)
        quantize_slab(2, 0)
        for m in range(HEAD_TILES):
            turn_and_read(m, GRAD)
        load_grad(5)
        load_wa(2, 1)
        load_wb_scales(scales_last, (2,))
        load_wb((2,), b_passes)
        load_resid(6, (0, 1))
        load_grad(6)
        spread_gamma((0, 1))
        read_gamma((0, 1))
        weigh_slab(2, 1)
        quantize_slab(2, 1)
        quantize_wa(0, 1)
        multiply_head_b(2)

        for m in range(HEAD_TILES):
            quantize_slab(m, GRAD)
        multiply(0, 0, a_passes)
        multiply(1, 0, a_passes)
        regroup_wa(nc.scalar.copy, 1, 0, whole)
        regroup_wa(nc.scalar.copy, 1, 1, low)
        regroup_wa(nc.vector.tensor_copy, 1, 1, high)
        scale_and_store(0, 0)
        scale_and_store(1, 0)
        quantize_wa(1, 0)
        for j in range(SLABS):
            turn_and_read(HEAD_TILES, j)
        load_resid(7, (0, 1))
        load_grad(7)
        quantize_wa(1, 1)
        unscaled = [(2, 0), (0, 1), (1, 1), (2, 1)]
        for unit in unscaled:
            multiply(*unit, a_passes)
        weigh_slab(HEAD_TILES, 0)
        weigh_slab(HEAD_TILES, 1)
        for j in range(SLABS):
            quantize_slab(HEAD_TILES, j)

        last_col = COL_TILES - 1
        rounded_batches = []
        read_batches = []
        for m in range(HEAD_TILES, ROW_TILES - 1):
            units = [(m, 0), (m, 1)] + ([(m - LAG, last_col)] if m >= LAG else [])
            for j in range(SLABS):
                turn_slab(m + 1, j)
            turned_batches = rounded_batches
            for batch in turned_batches:
                turn_batch(batch)
            if m == LAG:
                spread_gamma((last_col,))
            scale_and_store(*unscaled[0])
            rounded_batches = take_waiting(max(0, m - LAG))
            for j in range(SLABS):
                read_slab(m + 1, j)
            if m == LAG:
                read_gamma((last_col,))
            for batch in turned_batches:
                read_batch(batch)
            for batch in rounded_batches:
                round_batch(nc.scalar.copy, batch)
            if m == LAG - 1:
                for g in range(A_PASSES):
                    regroup_wa(nc.scalar.copy, last_col, g, whole)
            if SORT_FROM <= m + 2 < ROW_TILES:
                for j in range(SLABS):
                    sort_slab(m + 2, j)
            for unit in units:
                multiply(*unit, all_passes)
            for batch in read_batches:
                quantize_batch(batch)
            read_batches = turned_batches
            weigh_slab(m + 1, 0)
            weigh_slab(m + 1, 1)
            quantize_slab(m + 1, 0)
            later = unscaled[1:] + units[:-1]
            scale_and_store(*later[0])
            quantize_slab(m + 1, 1)
            quantize_slab(m + 1, GRAD)
            for unit in later[1:]:
                scale_and_store(*unit)
            if m == LAG - 1:
                for g in range(A_PASSES):
                    quantize_wa(last_col, g)
            unscaled = units[-1:]

        m = ROW_TILES - 1
        behind = [(row, last_col) for row in range(m - LAG, ROW_TILES)]
        for units in ([(m, 0), (m, 1), behind[0]], behind[1:-1], behind[-1:]):
            turned_batches = rounded_batches
            for batch in turned_batches:
                turn_batch(batch)
            scale_and_store(*unscaled[0])
            rounded_batches = take_waiting(LATE_BATCHES)
            for batch in turned_batches:
                read_batch(batch)
            for unit in units:
                multiply(*unit, all_passes)
            for batch in read_batches:
                quantize_batch(batch)
            read_batches = []
            for batch in rounded_batches:
                round_batch(nc.vector.tensor_copy, batch)
            for batch in turned_batches:
                quantize_batch(batch)
            for unit in units[:-1]:
                scale_and_store(*unit)
            for batch in take_waiting(LATE_BATCHES - len(rounded_batches)):
                round_batch(nc.vector.tensor_copy, batch)
                rounded_batches.append(batch)
            unscaled = units[-1:]

        rounded_batches.append(round_last_unit(*unscaled[0]))
        scale_and_store(*unscaled[0])
        for batch in rounded_batches:
            turn_batch(batch)
            read_batch(batch)
            quantize_batch(batch)
